import numpy as np
import ml_dtypes


def mxq(x, axis, fmt="e4m3"):
    dtype, down = {"e4m3": (ml_dtypes.float8_e4m3fn, 7), "e5m2": (ml_dtypes.float8_e5m2, 14)}[fmt]
    v = np.moveaxis(np.asarray(x, np.float32).astype(ml_dtypes.bfloat16).astype(np.float64), axis, -1)
    blocks = v.reshape(v.shape[:-1] + (-1, 32))
    amax = np.abs(blocks).max(-1, keepdims=True)
    byte = np.maximum(np.where(amax > 0, np.frexp(amax)[1] - 1 + 127, 0) - down, 1)
    scale = np.exp2(byte - 127.0)
    codes = (blocks / scale).astype(np.float32).astype(dtype).astype(np.float64)
    return np.moveaxis((codes * scale).reshape(v.shape), -1, axis)


WIDE = False


def mx_kscale(k):
    if not WIDE:
        return np.ones(k)
    levels = np.array([10, -10, 5, -5, 0])
    if k % 512:
        return np.exp2(np.random.permutation(np.resize(levels, k // 32))).repeat(32)
    a = np.empty((k // 512, 16))
    for p in range(k // 512):
        a[p, :8] = np.random.permutation(np.resize(levels, 8))
        for g in range(8):
            far = levels[np.abs(levels - a[p, g]) >= 10]
            a[p, g + 8] = far[np.random.randint(len(far))]
    return np.exp2(a.ravel()).repeat(32)


def f64(x):
    return np.asarray(x).astype(np.float64)


def striped(idx):
    return np.tile(idx.reshape(-1, 16).T, (8, 1)).astype(np.uint16)


def unstriped(offs):
    return offs[:16].T.reshape(-1).astype(np.int64)


def striped8(idx):
    return np.concatenate([x.reshape(-1, 16).T for x in idx]).astype(np.uint16)


def runs(offs, k):
    lists = np.stack([offs[16 * r : 16 * r + 16].T.reshape(-1) for r in range(8)]).astype(np.int64)
    return lists[np.arange(k) % 512 // 64]


def pack_weight(w):
    k, n = w.shape
    w = f64(np.asarray(w, np.float32).astype(ml_dtypes.bfloat16)).reshape(k // 32, 32, n)
    amax = np.abs(w).max(1)
    byte = np.clip(np.where(amax > 0, np.frexp(amax)[1] - 1 + 127 - 7, 1), 1, 254)
    scaled = (w * np.exp2(127.0 - byte)[:, None, :]).reshape(k, n).astype(np.float32)
    words = np.ascontiguousarray(scaled.reshape(k // 512, 128, 4, n).transpose(0, 1, 3, 2)).astype(ml_dtypes.float8_e4m3fn).view(np.uint8)
    return words, np.ascontiguousarray(byte.astype(np.uint8).reshape(k // 512, 16, n))


def unpack_weight(words, scales):
    g, p, n, _ = words.shape
    vals = np.ascontiguousarray(words).view(ml_dtypes.float8_e4m3fn).astype(np.float64) * np.repeat(np.exp2(scales.astype(np.float64) - 127.0), 8, axis=1)[..., None]
    return vals.transpose(0, 1, 3, 2).reshape(g * 512, n)

def planes(y):
    n, m = y.shape
    v = y.astype(np.float32).astype(ml_dtypes.bfloat16).astype(np.float64).reshape(n // 32, 32, m)
    top = np.abs(v).max(1)
    byte = np.clip(np.where(top > 0, np.frexp(top)[1] - 1 + 127 - 7, 1), 1, 254)
    codes = (v * np.exp2(127.0 - byte)[:, None, :]).reshape(n, m).astype(np.float32).astype(ml_dtypes.float8_e4m3fn).view(np.uint8)
    words = codes.reshape(n // 512, 128, 4, m).transpose(0, 1, 3, 2)
    return np.ascontiguousarray(words), np.ascontiguousarray(byte.astype(np.uint8).reshape(n // 512, 16, m))


K, T, S, H = 512, 2048, 512, 512
P = 2 ** 7


def setup_inputs():
    n = np.random.standard_normal
    s = mx_kscale(K)[:, None]
    u = mx_kscale(H)
    packed_xT = pack_weight(n((K, T)) * s)
    return {
        "x_words": packed_xT[0],
        "x_scales": packed_xT[1],
        "w1": (n((K, H)) / np.sqrt(K) / s * u).astype(np.float32),
        "w2": (n((H, H)) / np.sqrt(H) / u[:, None] * u).astype(np.float32),
        "om": np.tile(np.random.uniform(0.5, 1.5, S), (P, 1)).astype(np.float32),
        "offs": striped(np.random.permutation(T)[:S]),
        "stream": striped8(np.stack([np.random.permutation(S) for _ in range(8)])),
    }


def reference(x_words, x_scales, w1, w2, om, offs, stream):
    xq = unpack_weight(x_words, x_scales)[:, unstriped(offs)]
    y = mxq(f64(w1), 0, "e4m3").T @ xq
    z = y[np.arange(H)[:, None], runs(stream, H)]
    eq = mxq(f64(w2), 0, "e4m3").T @ mxq(z, 0, "e4m3")
    out_0 = z + f64(om)[:1] * (eq - z)
    return (out_0,) + planes(out_0)

@@ -1,0 +1,216 @@
+from contextlib import ExitStack
+
+import concourse.mybir as mybir
+from concourse.masks import make_identity
+
+F32 = mybir.dt.float32
+BF16 = mybir.dt.bfloat16
+I32 = mybir.dt.int32
+U32 = mybir.dt.uint32
+U16 = mybir.dt.uint16
+U8 = mybir.dt.uint8
+FP8X4 = mybir.dt.float8_e4m3fn_x4
+MULT = mybir.AluOpType.mult
+ADD = mybir.AluOpType.add
+
+P = 128
+K, T, S, H = 512, 2048, 512, 512
+FLOPS = 2 * 2 * 512 * 512 * 512
+COPY = mybir.ActivationFunctionType.Copy
+
+
+def tile_picked_lbm8_none_po_kernel(
+    tc, x_words, x_scales, w1, w2, om, offs, stream, out_0, out_1, out_2
+):
+    nc = tc.nc
+    with ExitStack() as ctx:
+        keep = ctx.enter_context(tc.tile_pool(name="keep", bufs=1))
+        shared = ctx.enter_context(tc.tile_pool(name="shared", bufs=1))
+        psum = ctx.enter_context(tc.psum_pool(name="psum", bufs=8))
+
+        def placed(shape, dtype, name, kib):
+            return shared.tile(shape, dtype, name=name, offset=1024 * kib, align_bytes=64)
+
+        offs_t = keep.tile([P, S // 16], U16, name="offs_t")
+        stream_t = keep.tile([P, S // 16], U16, name="stream_t")
+        xw = keep.tile([P, T], I32, name="xw")
+        xs = placed([P, T], U8, "xs", 0)
+        w1_raw = placed([P, 4, H], F32, "w1_raw", 2)
+        om_t = keep.tile([P, S], F32, name="om_t")
+        omc = keep.tile([P, S], F32, name="omc")
+        om_col = keep.tile([P, 4], F32, name="om_col")
+        ident = keep.tile([P, P], F32, name="ident")
+
+        nc.vector.memset(xs[:].bitcast(I32), 0)
+        nc.sync.dma_start(offs_t[:], offs)
+        nc.sync.dma_start(w1_raw[:], w1.rearrange("(p j) c -> p j c", j=4))
+        for q in range(4):
+            nc.sync.dma_start(
+                xs[32 * q : 32 * q + 4, :].bitcast(I32), x_scales[0, 4 * q : 4 * q + 4, :].bitcast(I32)
+            )
+        nc.sync.dma_start(xw[:], x_words[0].rearrange("p n t -> p (n t)").bitcast(I32))
+        nc.sync.dma_start(stream_t[:], stream)
+        nc.sync.dma_start(om_t[:], om)
+        make_identity(nc, ident[:])
+
+        xg_s = keep.tile([P, S], U8, name="xg_s", align_bytes=64)
+        nc.vector.tensor_copy(xg_s[:], xs[:].indirect(offs_t[:]))
+
+        def deal(engine_copy, u):
+            grouped = keep.tile([P, 2, P, 4], BF16, name=f"w1g{u}", align_bytes=64)
+            engine_copy(
+                grouped[:].rearrange("p t m j -> p m j t"),
+                w1_raw[:].rearrange("p j (m t) -> p m j t", t=4)[:, :, :, 2 * u : 2 * u + 2],
+            )
+            return grouped
+
+        def quant(grouped_flat, width, name):
+            codes = keep.tile([P, width], U32, name=name + "_c", align_bytes=64)
+            scales = keep.tile([P, width], U8, name=name + "_s", align_bytes=64)
+            nc.vector.quantize_mx(out=codes[:].bitcast(FP8X4), scales=scales[:], in_=grouped_flat)
+            return codes, scales
+
+        def interleave(engine_copy, dst, src):
+            engine_copy(dst.rearrange("p (c i) t -> p c t i", i=4), src.rearrange("p t (c i) -> p c t i", i=4))
+
+        w1g = [deal(nc.vector.tensor_copy, 0), deal(lambda a, b: nc.scalar.activation(a, b, COPY), 1)]
+        w1q = [quant(w1g[u][:].rearrange("p t m j -> p (t m j)"), 256, f"w1q{u}") for u in range(2)]
+
+        w2_raw = placed([P, 4, H], F32, "w2_raw", 2)
+        nc.sync.dma_start(w2_raw[:], w2.rearrange("(p j) c -> p j c", j=4))
+
+        xg = [placed([P, 256], U32, f"xg{h}", h) for h in range(2)]
+        for h in range(2):
+            nc.vector.tensor_copy(xg[h][:], xw[:].bitcast(U32).indirect(offs_t[:, 16 * h : 16 * h + 16]))
+        nc.vector.tensor_scalar(omc[:], om_t[:], -1.0, 1.0, MULT, ADD)
+
+        y = [keep.tile([P, S], F32, name=f"y{t}") for t in range(4)]
+        for t, h in ((0, 0), (1, 0), (0, 1), (1, 1), (2, 0), (2, 1), (3, 0), (3, 1)):
+            u, e = divmod(t, 2)
+            acc = psum.tile([P, 512], F32, name="acc")
+            nc.tensor.matmul_mx(
+                out=acc[:, 0:256],
+                lhsT=w1q[u][0][:, P * e : P * e + P].bitcast(FP8X4),
+                lhsT_scale=w1q[u][1][:, P * e : P * e + P],
+                rhs=xg[h][:].bitcast(FP8X4),
+                rhs_scale=xg_s[:, 256 * h : 256 * h + 256],
+                start=True,
+                stop=True,
+            )
+            leave = nc.vector.tensor_copy if (t, h) == (0, 1) else nc.scalar.copy
+            leave(y[t][:, 256 * h : 256 * h + 256], acc[:, 0:256])
+
+        om_ps = psum.tile([P, 512], F32, name="acc")
+        for q in range(4):
+            nc.tensor.transpose(om_ps[:, P * q : P * q + P], om_t[:, P * q : P * q + P], ident[:])
+        w2g = placed([P, H, 4], BF16, "w2g", 10)
+        for u in range(2):
+            interleave(nc.scalar.copy, w2g[:, 256 * u : 256 * u + 256, :], w2_raw[:, :, 256 * u : 256 * u + 256])
+        nc.scalar.copy(om_col[:], om_ps[:, 0:512:P])
+
+        o_scales = keep.tile([P, S], U8, name="o_scales", align_bytes=64)
+        out0_v = out_0.rearrange("(p t) j -> p t j", t=4)
+        out1_v = out_1[0].rearrange("p n t -> p (n t)").bitcast(I32)
+
+        pieces = ((0, 256), (256, 128), (384, 128))
+        quarters = ((0, 0), (0, 128), (1, 0), (2, 0))
+        z, zb, zq, zc, eq_t, a_t, back, outs = {}, {}, {}, {}, {}, {}, {}, {}
+
+        def gather(i, planes):
+            a, n = pieces[i]
+            for t in planes:
+                nc.vector.tensor_copy(z[i][:, t, :], y[t][:].indirect(stream_t[:, a // 16 : (a + n) // 16]))
+
+        def round_z(i):
+            interleave(nc.scalar.copy, zb[i][:], z[i][:])
+
+        def quant_z(i):
+            zq[i] = quant(zb[i][:].rearrange("p n t -> p (n t)"), pieces[i][1], f"zq{i}")
+
+        def kept_share(i):
+            a, n = pieces[i]
+            nc.vector.tensor_tensor(zc[i][:], z[i][:], omc[:, a : a + n].unsqueeze(1).to_broadcast([P, 4, n]), MULT)
+
+        def product(q):
+            i, b = quarters[q]
+            eq_t[q] = psum.tile([P, 512], F32, name="acc")
+            nc.tensor.matmul_mx(
+                out=eq_t[q][:],
+                lhsT=zq[i][0][:, b : b + P].bitcast(FP8X4),
+                lhsT_scale=zq[i][1][:, b : b + P],
+                rhs=w2q[0][:].bitcast(FP8X4),
+                rhs_scale=w2q[1][:],
+                start=True,
+                stop=True,
+            )
+
+        def rate(q):
+            a_t[q] = keep.tile([P, 4, P], F32, name=f"a_t{q}")
+            nc.scalar.activation(
+                a_t[q][:], eq_t[q][:].rearrange("p (m t) -> p t m", t=4), COPY, scale=om_col[:, q : q + 1]
+            )
+
+        def turn(q):
+            back[q] = psum.tile([P, 512], F32, name="acc")
+            for t in range(4):
+                nc.tensor.transpose(back[q][:, P * t : P * t + P], a_t[q][:, t, :], ident[:])
+
+        def add(q):
+            i, b = quarters[q]
+            outs[q] = keep.tile([P, 4, P], F32, name=f"o{q}")
+            nc.vector.tensor_tensor(
+                outs[q][:], back[q][:].rearrange("p (t j) -> p t j", t=4), zc[i][:, :, b : b + P], ADD
+            )
+            nc.sync.dma_start(out0_v[:, :, q * P : q * P + P], outs[q][:])
+
+        def hand_on(q, engine_copy):
+            a = q * P
+            ob = keep.tile([P, P, 4], BF16, name=f"ob{q}", align_bytes=64)
+            interleave(engine_copy, ob[:], outs[q][:])
+            codes = keep.tile([P, P], I32, name=f"oc{q}", align_bytes=64)
+            nc.vector.quantize_mx(
+                out=codes[:].bitcast(FP8X4), scales=o_scales[:, a : a + P], in_=ob[:].rearrange("p n t -> p (n t)")
+            )
+            nc.sync.dma_start(out1_v[:, a : a + P], codes[:])
+
+        z[0] = keep.tile([P, 4, 256], F32, name="z0")
+        z[1] = keep.tile([P, 4, 128], F32, name="z1")
+        gather(0, range(4))
+        gather(1, range(4))
+        w2q = quant(w2g[:].rearrange("p n t -> p (n t)"), H, "w2q")
+        zb[0] = placed([P, 256, 4], BF16, "zb0", 2)
+        zb[1] = placed([P, 128, 4], BF16, "zb1", 6)
+        zb[2] = placed([P, 128, 4], BF16, "zb2", 8)
+        round_z(0)
+        round_z(1)
+        z[2] = placed([P, 4, 128], F32, "z2", 10)
+        gather(2, (0, 1))
+        quant_z(0)
+        product(0)
+        product(1)
+        gather(2, (2, 3))
+        quant_z(1)
+        product(2)
+        round_z(2)
+        zc[0] = placed([P, 4, 256], F32, "zc0", 2)
+        kept_share(0)
+        quant_z(2)
+        product(3)
+        zc[1] = placed([P, 4, 128], F32, "zc1", 6)
+        zc[2] = placed([P, 4, 128], F32, "zc2", 8)
+        for q in range(4):
+            rate(q)
+        for q in range(4):
+            turn(q)
+        kept_share(1)
+        add(0)
+        add(1)
+        kept_share(2)
+        add(2)
+        add(3)
+        for q, engine_copy in enumerate((nc.scalar.copy, nc.scalar.copy, nc.scalar.copy, nc.vector.tensor_copy)):
+            hand_on(q, engine_copy)
+        for q in range(4):
+            (nc.scalar, nc.sync)[q % 2].dma_start(
+                out_2[0, 4 * q : 4 * q + 4, :].bitcast(I32), o_scales[32 * q : 32 * q + 4, :].bitcast(I32)
+            )

@@ -37,7 +37,7 @@ def tile_picked_lbm8_none_po_kernel(
         xs = placed([P, T], U8, "xs", 0)
         w1_raw = placed([P, 4, H], F32, "w1_raw", 2)
         om_t = keep.tile([P, S], F32, name="om_t")
-        omc = keep.tile([P, S], F32, name="omc")
+        omc_col = keep.tile([P, 4], F32, name="omc_col")
         om_col = keep.tile([P, 4], F32, name="om_col")
         ident = keep.tile([P, P], F32, name="ident")
 
@@ -82,7 +82,6 @@ def tile_picked_lbm8_none_po_kernel(
         xg = [placed([P, 256], U32, f"xg{h}", h) for h in range(2)]
         for h in range(2):
             nc.vector.tensor_copy(xg[h][:], xw[:].bitcast(U32).indirect(offs_t[:, 16 * h : 16 * h + 16]))
-        nc.vector.tensor_scalar(omc[:], om_t[:], -1.0, 1.0, MULT, ADD)
 
         y = [keep.tile([P, S], F32, name=f"y{t}") for t in range(4)]
         for t, h in ((0, 0), (1, 0), (0, 1), (1, 1), (2, 0), (2, 1), (3, 0), (3, 1)):
@@ -103,33 +102,38 @@ def tile_picked_lbm8_none_po_kernel(
         om_ps = psum.tile([P, 512], F32, name="acc")
         for q in range(4):
             nc.tensor.transpose(om_ps[:, P * q : P * q + P], om_t[:, P * q : P * q + P], ident[:])
-        w2g = placed([P, H, 4], BF16, "w2g", 10)
+        nc.vector.tensor_copy(om_col[:], om_ps[:, 0:512:P])
+        nc.vector.tensor_scalar(omc_col[:], om_ps[:, 0:512:P], -1.0, 1.0, MULT, ADD)
+        w2g = keep.tile([P, H, 4], BF16, name="w2g", align_bytes=64)
         for u in range(2):
             interleave(nc.scalar.copy, w2g[:, 256 * u : 256 * u + 256, :], w2_raw[:, :, 256 * u : 256 * u + 256])
-        nc.scalar.copy(om_col[:], om_ps[:, 0:512:P])
 
         o_scales = keep.tile([P, S], U8, name="o_scales", align_bytes=64)
         out0_v = out_0.rearrange("(p t) j -> p t j", t=4)
         out1_v = out_1[0].rearrange("p n t -> p (n t)").bitcast(I32)
 
-        pieces = ((0, 256), (256, 128), (384, 128))
-        quarters = ((0, 0), (0, 128), (1, 0), (2, 0))
-        z, zb, zq, zc, eq_t, a_t, back, outs = {}, {}, {}, {}, {}, {}, {}, {}
+        pieces = ((0, 128), (128, 256), (384, 128))
+        quarters = ((0, 0), (1, 0), (1, 128), (2, 0))
+        z, zb, zq, u_t, eq_t, o_t, back, outs = {}, {}, {}, {}, {}, {}, {}, {}
 
         def gather(i, planes):
             a, n = pieces[i]
             for t in planes:
                 nc.vector.tensor_copy(z[i][:, t, :], y[t][:].indirect(stream_t[:, a // 16 : (a + n) // 16]))
 
-        def round_z(i):
-            interleave(nc.scalar.copy, zb[i][:], z[i][:])
+        def round_z(i, engine_copy):
+            interleave(engine_copy, zb[i][:], z[i][:])
 
         def quant_z(i):
             zq[i] = quant(zb[i][:].rearrange("p n t -> p (n t)"), pieces[i][1], f"zq{i}")
 
-        def kept_share(i):
-            a, n = pieces[i]
-            nc.vector.tensor_tensor(zc[i][:], z[i][:], omc[:, a : a + n].unsqueeze(1).to_broadcast([P, 4, n]), MULT)
+        def kept_share(q, kib):
+            i, b = quarters[q]
+            z_t = psum.tile([P, 512], F32, name="acc")
+            for t in range(4):
+                nc.tensor.transpose(z_t[:, P * t : P * t + P], z[i][:, t, b : b + P], ident[:])
+            u_t[q] = placed([P, 512], F32, f"u_t{q}", kib)
+            nc.scalar.activation(u_t[q][:], z_t[:], COPY, scale=omc_col[:, q : q + 1])
 
         def product(q):
             i, b = quarters[q]
@@ -144,72 +148,75 @@ def tile_picked_lbm8_none_po_kernel(
                 stop=True,
             )
 
-        def rate(q):
-            a_t[q] = keep.tile([P, 4, P], F32, name=f"a_t{q}")
-            nc.scalar.activation(
-                a_t[q][:], eq_t[q][:].rearrange("p (m t) -> p t m", t=4), COPY, scale=om_col[:, q : q + 1]
+        def relax(q):
+            o_t[q] = keep.tile([P, 4, P], F32, name=f"o_t{q}")
+            nc.vector.scalar_tensor_tensor(
+                o_t[q][:],
+                eq_t[q][:].rearrange("p (m t) -> p t m", t=4),
+                om_col[:, q : q + 1],
+                u_t[q][:].rearrange("p (t m) -> p t m", t=4),
+                MULT,
+                ADD,
             )
 
         def turn(q):
             back[q] = psum.tile([P, 512], F32, name="acc")
             for t in range(4):
-                nc.tensor.transpose(back[q][:, P * t : P * t + P], a_t[q][:, t, :], ident[:])
+                nc.tensor.transpose(back[q][:, P * t : P * t + P], o_t[q][:, t, :], ident[:])
 
-        def add(q):
-            i, b = quarters[q]
+        def leave_psum(q):
             outs[q] = keep.tile([P, 4, P], F32, name=f"o{q}")
-            nc.vector.tensor_tensor(
-                outs[q][:], back[q][:].rearrange("p (t j) -> p t j", t=4), zc[i][:, :, b : b + P], ADD
-            )
+            nc.scalar.copy(outs[q][:], back[q][:].rearrange("p (t j) -> p t j", t=4))
             nc.sync.dma_start(out0_v[:, :, q * P : q * P + P], outs[q][:])
 
-        def hand_on(q, engine_copy):
+        def hand_on(q, from_psum):
             a = q * P
             ob = keep.tile([P, P, 4], BF16, name=f"ob{q}", align_bytes=64)
-            interleave(engine_copy, ob[:], outs[q][:])
+            if from_psum:
+                nc.vector.tensor_copy(ob[:], back[q][:].rearrange("p (t j) -> p j t", t=4))
+            else:
+                interleave(nc.vector.tensor_copy, ob[:], outs[q][:])
             codes = keep.tile([P, P], I32, name=f"oc{q}", align_bytes=64)
             nc.vector.quantize_mx(
                 out=codes[:].bitcast(FP8X4), scales=o_scales[:, a : a + P], in_=ob[:].rearrange("p n t -> p (n t)")
             )
             nc.sync.dma_start(out1_v[:, a : a + P], codes[:])
 
-        z[0] = keep.tile([P, 4, 256], F32, name="z0")
-        z[1] = keep.tile([P, 4, 128], F32, name="z1")
+        z[0] = keep.tile([P, 4, 128], F32, name="z0")
+        z[1] = keep.tile([P, 4, 256], F32, name="z1")
         gather(0, range(4))
         gather(1, range(4))
         w2q = quant(w2g[:].rearrange("p n t -> p (n t)"), H, "w2q")
-        zb[0] = placed([P, 256, 4], BF16, "zb0", 2)
-        zb[1] = placed([P, 128, 4], BF16, "zb1", 6)
-        zb[2] = placed([P, 128, 4], BF16, "zb2", 8)
-        round_z(0)
-        round_z(1)
-        z[2] = placed([P, 4, 128], F32, "z2", 10)
-        gather(2, (0, 1))
+        zb[0] = placed([P, 128, 4], BF16, "zb0", 2)
+        zb[1] = placed([P, 256, 4], BF16, "zb1", 3)
+        zb[2] = keep.tile([P, 128, 4], BF16, name="zb2", align_bytes=64)
+        round_z(0, nc.scalar.copy)
         quant_z(0)
         product(0)
-        product(1)
-        gather(2, (2, 3))
+        round_z(1, nc.scalar.copy)
+        kept_share(0, 5)
+        z[2] = placed([P, 4, 128], F32, "z2", 1)
+        gather(2, range(4))
+        round_z(2, nc.scalar.copy)
+        kept_share(1, 7)
+        kept_share(2, 9)
+        kept_share(3, 11)
         quant_z(1)
+        product(1)
         product(2)
-        round_z(2)
-        zc[0] = placed([P, 4, 256], F32, "zc0", 2)
-        kept_share(0)
+        relax(0)
         quant_z(2)
         product(3)
-        zc[1] = placed([P, 4, 128], F32, "zc1", 6)
-        zc[2] = placed([P, 4, 128], F32, "zc2", 8)
-        for q in range(4):
-            rate(q)
+        for q in range(1, 4):
+            relax(q)
         for q in range(4):
             turn(q)
-        kept_share(1)
-        add(0)
-        add(1)
-        kept_share(2)
-        add(2)
-        add(3)
-        for q, engine_copy in enumerate((nc.scalar.copy, nc.scalar.copy, nc.scalar.copy, nc.vector.tensor_copy)):
-            hand_on(q, engine_copy)
+        for q in range(3):
+            leave_psum(q)
+        for q in range(3):
+            hand_on(q, False)
+        hand_on(3, True)
+        leave_psum(3)
         for q in range(4):
             (nc.scalar, nc.sync)[q % 2].dma_start(
                 out_2[0, 4 * q : 4 * q + 4, :].bitcast(I32), o_scales[32 * q : 32 * q + 4, :].bitcast(I32)

@@ -36,9 +36,7 @@ def tile_picked_lbm8_none_po_kernel(
         xw = keep.tile([P, T], I32, name="xw")
         xs = placed([P, T], U8, "xs", 0)
         w1_raw = placed([P, 4, H], F32, "w1_raw", 2)
-        om_t = keep.tile([P, S], F32, name="om_t")
-        omc_col = keep.tile([P, 4], F32, name="omc_col")
-        om_col = keep.tile([P, 4], F32, name="om_col")
+        keep_rate = keep.tile([P, P + 4], F32, name="keep_rate")
         ident = keep.tile([P, P], F32, name="ident")
 
         nc.vector.memset(xs[:].bitcast(I32), 0)
@@ -46,18 +44,17 @@ def tile_picked_lbm8_none_po_kernel(
         nc.sync.dma_start(w1_raw[:], w1.rearrange("(p j) c -> p j c", j=4))
         for q in range(4):
             nc.sync.dma_start(
-                xs[32 * q : 32 * q + 4, :].bitcast(I32), x_scales[0, 4 * q : 4 * q + 4, :].bitcast(I32)
+                xs[q:P:32, :].bitcast(I32), x_scales[0, q:16:4, :].bitcast(I32)
             )
         nc.sync.dma_start(xw[:], x_words[0].rearrange("p n t -> p (n t)").bitcast(I32))
         nc.sync.dma_start(stream_t[:], stream)
-        nc.sync.dma_start(om_t[:], om)
         make_identity(nc, ident[:])
 
         xg_s = keep.tile([P, S], U8, name="xg_s", align_bytes=64)
         nc.vector.tensor_copy(xg_s[:], xs[:].indirect(offs_t[:]))
 
         def deal(engine_copy, u):
-            grouped = keep.tile([P, 2, P, 4], BF16, name=f"w1g{u}", align_bytes=64)
+            grouped = placed([P, 2, P, 4], BF16, f"w1g{u}", 13 + 2 * u)
             engine_copy(
                 grouped[:].rearrange("p t m j -> p m j t"),
                 w1_raw[:].rearrange("p j (m t) -> p m j t", t=4)[:, :, :, 2 * u : 2 * u + 2],
@@ -79,6 +76,11 @@ def tile_picked_lbm8_none_po_kernel(
         w2_raw = placed([P, 4, H], F32, "w2_raw", 2)
         nc.sync.dma_start(w2_raw[:], w2.rearrange("(p j) c -> p j c", j=4))
 
+        rate = placed([P, P + 4], F32, "rate", 15)
+        nc.sync.dma_start(rate[:, 0:P], om[:, 3 * P : 4 * P])
+        with nc.allow_non_contiguous_dma(reason="one rate for each partition"):
+            nc.sync.dma_start(rate[:, P : P + 4], om[0].rearrange("(q p) -> p q", p=P))
+
         xg = [placed([P, 256], U32, f"xg{h}", h) for h in range(2)]
         for h in range(2):
             nc.vector.tensor_copy(xg[h][:], xw[:].bitcast(U32).indirect(offs_t[:, 16 * h : 16 * h + 16]))
@@ -96,17 +98,11 @@ def tile_picked_lbm8_none_po_kernel(
                 start=True,
                 stop=True,
             )
-            leave = nc.vector.tensor_copy if (t, h) == (0, 1) else nc.scalar.copy
+            leave = nc.vector.tensor_copy if t == 0 else nc.scalar.copy
             leave(y[t][:, 256 * h : 256 * h + 256], acc[:, 0:256])
 
-        om_ps = psum.tile([P, 512], F32, name="acc")
-        for q in range(4):
-            nc.tensor.transpose(om_ps[:, P * q : P * q + P], om_t[:, P * q : P * q + P], ident[:])
-        nc.vector.tensor_copy(om_col[:], om_ps[:, 0:512:P])
-        nc.vector.tensor_scalar(omc_col[:], om_ps[:, 0:512:P], -1.0, 1.0, MULT, ADD)
-        w2g = keep.tile([P, H, 4], BF16, name="w2g", align_bytes=64)
-        for u in range(2):
-            interleave(nc.scalar.copy, w2g[:, 256 * u : 256 * u + 256, :], w2_raw[:, :, 256 * u : 256 * u + 256])
+        w2g = keep.tile([P, 4, P, 4], BF16, name="w2g", align_bytes=64)
+        nc.scalar.copy(w2g[:].rearrange("p t m j -> p m j t"), w2_raw[:].rearrange("p j (m t) -> p m j t", t=4))
 
         o_scales = keep.tile([P, S], U8, name="o_scales", align_bytes=64)
         out0_v = out_0.rearrange("(p t) j -> p t j", t=4)
@@ -114,6 +110,7 @@ def tile_picked_lbm8_none_po_kernel(
 
         pieces = ((0, 128), (128, 256), (384, 128))
         quarters = ((0, 0), (1, 0), (1, 128), (2, 0))
+        z_t = {}
         z, zb, zq, u_t, eq_t, o_t, back, outs = {}, {}, {}, {}, {}, {}, {}, {}
 
         def gather(i, planes):
@@ -127,13 +124,15 @@ def tile_picked_lbm8_none_po_kernel(
         def quant_z(i):
             zq[i] = quant(zb[i][:].rearrange("p n t -> p (n t)"), pieces[i][1], f"zq{i}")
 
-        def kept_share(q, kib):
+        def turn_z(q):
             i, b = quarters[q]
-            z_t = psum.tile([P, 512], F32, name="acc")
+            z_t[q] = psum.tile([P, 512], F32, name="acc")
             for t in range(4):
-                nc.tensor.transpose(z_t[:, P * t : P * t + P], z[i][:, t, b : b + P], ident[:])
+                nc.tensor.transpose(z_t[q][:, P * t : P * t + P], z[i][:, t, b : b + P], ident[:])
+
+        def kept_share(q, kib):
             u_t[q] = placed([P, 512], F32, f"u_t{q}", kib)
-            nc.scalar.activation(u_t[q][:], z_t[:], COPY, scale=omc_col[:, q : q + 1])
+            nc.scalar.activation(u_t[q][:], z_t[q][:], COPY, scale=keep_rate[:, P + q : P + q + 1])
 
         def product(q):
             i, b = quarters[q]
@@ -151,10 +150,10 @@ def tile_picked_lbm8_none_po_kernel(
         def relax(q):
             o_t[q] = keep.tile([P, 4, P], F32, name=f"o_t{q}")
             nc.vector.scalar_tensor_tensor(
-                o_t[q][:],
-                eq_t[q][:].rearrange("p (m t) -> p t m", t=4),
-                om_col[:, q : q + 1],
-                u_t[q][:].rearrange("p (t m) -> p t m", t=4),
+                o_t[q][:].rearrange("p t m -> p (t m)"),
+                eq_t[q][:],
+                rate[:, P + q : P + q + 1],
+                u_t[q][:],
                 MULT,
                 ADD,
             )
@@ -169,13 +168,10 @@ def tile_picked_lbm8_none_po_kernel(
             nc.scalar.copy(outs[q][:], back[q][:].rearrange("p (t j) -> p t j", t=4))
             nc.sync.dma_start(out0_v[:, :, q * P : q * P + P], outs[q][:])
 
-        def hand_on(q, from_psum):
+        def hand_on(q, engine_copy):
             a = q * P
             ob = keep.tile([P, P, 4], BF16, name=f"ob{q}", align_bytes=64)
-            if from_psum:
-                nc.vector.tensor_copy(ob[:], back[q][:].rearrange("p (t j) -> p j t", t=4))
-            else:
-                interleave(nc.vector.tensor_copy, ob[:], outs[q][:])
+            interleave(engine_copy, ob[:], outs[q][:])
             codes = keep.tile([P, P], I32, name=f"oc{q}", align_bytes=64)
             nc.vector.quantize_mx(
                 out=codes[:].bitcast(FP8X4), scales=o_scales[:, a : a + P], in_=ob[:].rearrange("p n t -> p (n t)")
@@ -186,38 +182,62 @@ def tile_picked_lbm8_none_po_kernel(
         z[1] = keep.tile([P, 4, 256], F32, name="z1")
         gather(0, range(4))
         gather(1, range(4))
-        w2q = quant(w2g[:].rearrange("p n t -> p (n t)"), H, "w2q")
+        nc.vector.tensor_scalar(keep_rate[:], rate[:], -1.0, 1.0, MULT, ADD)
+        w2q = quant(w2g[:].rearrange("p t m j -> p (t m j)"), H, "w2q")
         zb[0] = placed([P, 128, 4], BF16, "zb0", 2)
         zb[1] = placed([P, 256, 4], BF16, "zb1", 3)
-        zb[2] = keep.tile([P, 128, 4], BF16, name="zb2", align_bytes=64)
+        zb[2] = placed([P, 128, 4], BF16, "zb2", 11)
+        turn_z(0)
+        turn_z(1)
         round_z(0, nc.scalar.copy)
         quant_z(0)
         product(0)
+        turn_z(2)
         round_z(1, nc.scalar.copy)
         kept_share(0, 5)
         z[2] = placed([P, 4, 128], F32, "z2", 1)
         gather(2, range(4))
-        round_z(2, nc.scalar.copy)
-        kept_share(1, 7)
-        kept_share(2, 9)
-        kept_share(3, 11)
         quant_z(1)
         product(1)
         product(2)
         relax(0)
+        turn(0)
+        round_z(2, nc.scalar.copy)
+        kept_share(1, 7)
+        kept_share(2, 9)
         quant_z(2)
-        product(3)
-        for q in range(1, 4):
-            relax(q)
-        for q in range(4):
-            turn(q)
-        for q in range(3):
-            leave_psum(q)
-        for q in range(3):
-            hand_on(q, False)
-        hand_on(3, True)
-        leave_psum(3)
+        eq = psum.tile([P, 512], F32, name="acc")
+        for t in range(4):
+            nc.tensor.matmul_mx(
+                out=eq[:, P * t : P * t + P],
+                lhsT=w2q[0][:, P * t : P * t + P].bitcast(FP8X4),
+                lhsT_scale=w2q[1][:, P * t : P * t + P],
+                rhs=zq[2][0][:].bitcast(FP8X4),
+                rhs_scale=zq[2][1][:],
+                start=True,
+                stop=True,
+            )
+        leave_psum(0)
+        relax(1)
+        relax(2)
+        turn(1)
+        turn(2)
+        kept = placed([P, 4, P], F32, "kept", 11)
+        nc.vector.tensor_tensor(kept[:], z[2][:], keep_rate[:, 0:P].unsqueeze(1).to_broadcast([P, 4, P]), MULT)
+        leave_psum(1)
+        leave_psum(2)
+        moved = keep.tile([P, 4, P], F32, name="moved")
+        nc.vector.tensor_tensor(
+            moved[:], eq[:].rearrange("p (t j) -> p t j", t=4), rate[:, 0:P].unsqueeze(1).to_broadcast([P, 4, P]), MULT
+        )
+        outs[3] = keep.tile([P, 4, P], F32, name="o3")
+        nc.vector.tensor_tensor(outs[3][:], moved[:], kept[:], ADD)
+        nc.sync.dma_start(out0_v[:, :, 3 * P : 4 * P], outs[3][:])
+        hand_on(0, nc.scalar.copy)
+        hand_on(1, nc.scalar.copy)
+        hand_on(3, nc.vector.tensor_copy)
+        hand_on(2, nc.vector.tensor_copy)
         for q in range(4):
             (nc.scalar, nc.sync)[q % 2].dma_start(
-                out_2[0, 4 * q : 4 * q + 4, :].bitcast(I32), o_scales[32 * q : 32 * q + 4, :].bitcast(I32)
+                out_2[0, q:16:4, :].bitcast(I32), o_scales[q:P:32, :].bitcast(I32)
             )

@@ -33,19 +33,16 @@ def tile_picked_lbm8_none_po_kernel(
 
         offs_t = keep.tile([P, S // 16], U16, name="offs_t")
         stream_t = keep.tile([P, S // 16], U16, name="stream_t")
-        xw = keep.tile([P, T], I32, name="xw")
+        xw = placed([P, T], I32, "xw", 36)
         xs = placed([P, T], U8, "xs", 0)
         w1_raw = placed([P, 4, H], F32, "w1_raw", 2)
-        keep_rate = keep.tile([P, P + 4], F32, name="keep_rate")
         ident = keep.tile([P, P], F32, name="ident")
 
         nc.vector.memset(xs[:].bitcast(I32), 0)
-        nc.sync.dma_start(offs_t[:], offs)
         nc.sync.dma_start(w1_raw[:], w1.rearrange("(p j) c -> p j c", j=4))
+        nc.sync.dma_start(offs_t[:], offs)
         for q in range(4):
-            nc.sync.dma_start(
-                xs[q:P:32, :].bitcast(I32), x_scales[0, q:16:4, :].bitcast(I32)
-            )
+            nc.sync.dma_start(xs[q:P:32, :].bitcast(I32), x_scales[0, q:16:4, :].bitcast(I32))
         nc.sync.dma_start(xw[:], x_words[0].rearrange("p n t -> p (n t)").bitcast(I32))
         nc.sync.dma_start(stream_t[:], stream)
         make_identity(nc, ident[:])
@@ -53,16 +50,23 @@ def tile_picked_lbm8_none_po_kernel(
         xg_s = keep.tile([P, S], U8, name="xg_s", align_bytes=64)
         nc.vector.tensor_copy(xg_s[:], xs[:].indirect(offs_t[:]))
 
+        def scalar_copy(dst, src):
+            nc.scalar.activation(dst, src, COPY)
+
+        def gpsimd_copy(dst, src):
+            nc.gpsimd.tensor_scalar(dst, src, 1.0, 0.0, MULT, ADD)
+
         def deal(engine_copy, u):
-            grouped = placed([P, 2, P, 4], BF16, f"w1g{u}", 13 + 2 * u)
+            grouped = placed([P, 2, P, 4], BF16, f"w1g{u}", 10 + 2 * u)
             engine_copy(
                 grouped[:].rearrange("p t m j -> p m j t"),
                 w1_raw[:].rearrange("p j (m t) -> p m j t", t=4)[:, :, :, 2 * u : 2 * u + 2],
             )
             return grouped
 
-        def quant(grouped_flat, width, name):
-            codes = keep.tile([P, width], U32, name=name + "_c", align_bytes=64)
+        def quant(grouped_flat, width, name, codes=None):
+            if codes is None:
+                codes = keep.tile([P, width], U32, name=name + "_c", align_bytes=64)
             scales = keep.tile([P, width], U8, name=name + "_s", align_bytes=64)
             nc.vector.quantize_mx(out=codes[:].bitcast(FP8X4), scales=scales[:], in_=grouped_flat)
             return codes, scales
@@ -70,27 +74,45 @@ def tile_picked_lbm8_none_po_kernel(
         def interleave(engine_copy, dst, src):
             engine_copy(dst.rearrange("p (c i) t -> p c t i", i=4), src.rearrange("p t (c i) -> p c t i", i=4))
 
-        w1g = [deal(nc.vector.tensor_copy, 0), deal(lambda a, b: nc.scalar.activation(a, b, COPY), 1)]
-        w1q = [quant(w1g[u][:].rearrange("p t m j -> p (t m j)"), 256, f"w1q{u}") for u in range(2)]
+        w1g = [deal(nc.vector.tensor_copy, 0), deal(scalar_copy, 1)]
+        w1q = [
+            quant(w1g[0][:].rearrange("p t m j -> p (t m j)"), 256, "w1q0", placed([P, 256], U32, "w1q0_c", 0)),
+        ]
 
-        w2_raw = placed([P, 4, H], F32, "w2_raw", 2)
-        nc.sync.dma_start(w2_raw[:], w2.rearrange("(p j) c -> p j c", j=4))
+        w2_rows = w2.rearrange("(p j) c -> p j c", j=4)
+        w2_cuts = ((0, 256, 22), (256, 64, 26), (320, 192, 28))
+        w2_raw = [placed([P, 4, n], F32, f"w2_raw{h}", kib) for h, (a, n, kib) in enumerate(w2_cuts)]
+        for h, (a, n, kib) in enumerate(w2_cuts):
+            nc.sync.dma_start(w2_raw[h][:], w2_rows[:, :, a : a + n])
 
-        rate = placed([P, P + 4], F32, "rate", 15)
-        nc.sync.dma_start(rate[:, 0:P], om[:, 3 * P : 4 * P])
+        rate = keep.tile([P, 128 + 3], F32, name="rate")
+        nc.sync.dma_start(rate[:, 0:128], om[:, 384:512])
         with nc.allow_non_contiguous_dma(reason="one rate for each partition"):
-            nc.sync.dma_start(rate[:, P : P + 4], om[0].rearrange("(q p) -> p q", p=P))
+            nc.sync.dma_start(rate[:, 128:131], om[0, 0:384].rearrange("(q p) -> p q", p=P))
 
-        xg = [placed([P, 256], U32, f"xg{h}", h) for h in range(2)]
+        xg = [keep.tile([P, 256], U32, name="xg0", align_bytes=64), keep.tile([P, 256], U32, name="xg1", align_bytes=64)]
         for h in range(2):
             nc.vector.tensor_copy(xg[h][:], xw[:].bitcast(U32).indirect(offs_t[:, 16 * h : 16 * h + 16]))
+
+        w1q.append(quant(w1g[1][:].rearrange("p t m j -> p (t m j)"), 256, "w1q1", placed([P, 256], U32, "w1q1_c", 36)))
+        w2g = placed([P, 4, P, 4], BF16, "w2g", 32)
+
+        def deal_w2(engine_copy, h, walk):
+            a, n, kib = w2_cuts[h]
+            engine_copy(
+                w2g[:, :, a // 4 : (a + n) // 4, :].rearrange("p t m j -> " + walk),
+                w2_raw[h][:].rearrange("p j (m t) -> " + walk, t=4),
+            )
+
+        deal_w2(nc.vector.tensor_copy, 0, "p m j t")
 
         y = [keep.tile([P, S], F32, name=f"y{t}") for t in range(4)]
         for t, h in ((0, 0), (1, 0), (0, 1), (1, 1), (2, 0), (2, 1), (3, 0), (3, 1)):
             u, e = divmod(t, 2)
-            acc = psum.tile([P, 512], F32, name="acc")
+            if t < 2 or h == 0:
+                acc = psum.tile([P, 512], F32, name="acc")
             nc.tensor.matmul_mx(
-                out=acc[:, 0:256],
+                out=acc[:, 256 * h : 256 * h + 256],
                 lhsT=w1q[u][0][:, P * e : P * e + P].bitcast(FP8X4),
                 lhsT_scale=w1q[u][1][:, P * e : P * e + P],
                 rhs=xg[h][:].bitcast(FP8X4),
@@ -98,145 +120,184 @@ def tile_picked_lbm8_none_po_kernel(
                 start=True,
                 stop=True,
             )
-            leave = nc.vector.tensor_copy if t == 0 else nc.scalar.copy
-            leave(y[t][:, 256 * h : 256 * h + 256], acc[:, 0:256])
+            if t < 2:
+                nc.scalar.copy(y[t][:, 256 * h : 256 * h + 256], acc[:, 256 * h : 256 * h + 256])
+            elif h == 1:
+                nc.scalar.copy(y[t][:], acc[:])
 
-        w2g = keep.tile([P, 4, P, 4], BF16, name="w2g", align_bytes=64)
-        nc.scalar.copy(w2g[:].rearrange("p t m j -> p m j t"), w2_raw[:].rearrange("p j (m t) -> p m j t", t=4))
+        deal_w2(nc.scalar.copy, 1, "p m j t")
+        deal_w2(gpsimd_copy, 2, "p t m j")
+        keep_rate = keep.tile([P, 128 + 3], F32, name="keep_rate")
+        nc.gpsimd.tensor_scalar(keep_rate[:], rate[:], -1.0, 1.0, MULT, ADD)
 
         o_scales = keep.tile([P, S], U8, name="o_scales", align_bytes=64)
+        o_codes = [keep.tile([P, 256], I32, name=f"o_codes{h}", align_bytes=64) for h in range(2)]
         out0_v = out_0.rearrange("(p t) j -> p t j", t=4)
         out1_v = out_1[0].rearrange("p n t -> p (n t)").bitcast(I32)
 
-        pieces = ((0, 128), (128, 256), (384, 128))
-        quarters = ((0, 0), (1, 0), (1, 128), (2, 0))
-        z_t = {}
-        z, zb, zq, u_t, eq_t, o_t, back, outs = {}, {}, {}, {}, {}, {}, {}, {}
+        z01 = placed([P, 4, 256], F32, "z01", 22)
+        z, zb, zq, z_t, u_t, eq, o_t, back, outs, kept, moved, ob = ({} for i in range(12))
 
-        def gather(i, planes):
-            a, n = pieces[i]
-            for t in planes:
-                nc.vector.tensor_copy(z[i][:, t, :], y[t][:].indirect(stream_t[:, a // 16 : (a + n) // 16]))
+        def gather(dst, a, n):
+            for t in range(4):
+                nc.vector.tensor_copy(dst[:, t, :], y[t][:].indirect(stream_t[:, a // 16 : (a + n) // 16]))
 
-        def round_z(i, engine_copy):
-            interleave(engine_copy, zb[i][:], z[i][:])
+        def round_z(q, kib):
+            zb[q] = placed([P, P, 4], BF16, f"zb{q}", kib)
+            interleave(nc.scalar.copy, zb[q][:], z[q])
 
-        def quant_z(i):
-            zq[i] = quant(zb[i][:].rearrange("p n t -> p (n t)"), pieces[i][1], f"zq{i}")
+        def quant_z(q):
+            zq[q] = quant(zb[q][:].rearrange("p n t -> p (n t)"), P, f"zq{q}")
 
         def turn_z(q):
-            i, b = quarters[q]
             z_t[q] = psum.tile([P, 512], F32, name="acc")
             for t in range(4):
-                nc.tensor.transpose(z_t[q][:, P * t : P * t + P], z[i][:, t, b : b + P], ident[:])
+                nc.tensor.transpose(z_t[q][:, P * t : P * t + P], z[q][:, t, :], ident[:])
 
-        def kept_share(q, kib):
+        def kept_turned(q, kib):
             u_t[q] = placed([P, 512], F32, f"u_t{q}", kib)
-            nc.scalar.activation(u_t[q][:], z_t[q][:], COPY, scale=keep_rate[:, P + q : P + q + 1])
+            nc.scalar.activation(u_t[q][:], z_t[q][:], COPY, scale=keep_rate[:, 128 + q : 129 + q])
 
-        def product(q):
-            i, b = quarters[q]
-            eq_t[q] = psum.tile([P, 512], F32, name="acc")
+        def product_turned(q):
+            eq[q] = psum.tile([P, 512], F32, name="acc")
             nc.tensor.matmul_mx(
-                out=eq_t[q][:],
-                lhsT=zq[i][0][:, b : b + P].bitcast(FP8X4),
-                lhsT_scale=zq[i][1][:, b : b + P],
+                out=eq[q][:],
+                lhsT=zq[q][0][:].bitcast(FP8X4),
+                lhsT_scale=zq[q][1][:],
                 rhs=w2q[0][:].bitcast(FP8X4),
                 rhs_scale=w2q[1][:],
                 start=True,
                 stop=True,
             )
 
-        def relax(q):
+        def product_planes(q):
+            eq[q] = psum.tile([P, 512], F32, name="acc")
+            for t in range(4):
+                nc.tensor.matmul_mx(
+                    out=eq[q][:, P * t : P * t + P],
+                    lhsT=w2q[0][:, P * t : P * t + P].bitcast(FP8X4),
+                    lhsT_scale=w2q[1][:, P * t : P * t + P],
+                    rhs=zq[q][0][:].bitcast(FP8X4),
+                    rhs_scale=zq[q][1][:],
+                    start=True,
+                    stop=True,
+                )
+
+        def relax_turned(q):
             o_t[q] = keep.tile([P, 4, P], F32, name=f"o_t{q}")
             nc.vector.scalar_tensor_tensor(
-                o_t[q][:].rearrange("p t m -> p (t m)"),
-                eq_t[q][:],
-                rate[:, P + q : P + q + 1],
-                u_t[q][:],
-                MULT,
-                ADD,
+                o_t[q][:].rearrange("p t m -> p (t m)"), eq[q][:], rate[:, 128 + q : 129 + q], u_t[q][:], MULT, ADD
             )
 
-        def turn(q):
+        def moved_turned(q):
+            o_t[q] = keep.tile([P, 512], F32, name=f"e_t{q}")
+            nc.scalar.activation(o_t[q][:], eq[q][:], COPY, scale=rate[:, 128 + q : 129 + q])
+
+        def turn_back_sum(q):
+            back[q] = psum.tile([P, 512], F32, name="acc")
+            for t in range(4):
+                for first, part in ((True, u_t[q]), (False, o_t[q])):
+                    nc.tensor.matmul(
+                        back[q][:, P * t : P * t + P],
+                        part[:, P * t : P * t + P],
+                        ident[:],
+                        start=first,
+                        stop=not first,
+                        is_transpose=True,
+                    )
+
+        def turn_back(q):
             back[q] = psum.tile([P, 512], F32, name="acc")
             for t in range(4):
                 nc.tensor.transpose(back[q][:, P * t : P * t + P], o_t[q][:, t, :], ident[:])
 
+        def store(q):
+            nc.sync.dma_start(out0_v[:, :, q * P : q * P + P], outs[q][:])
+
         def leave_psum(q):
             outs[q] = keep.tile([P, 4, P], F32, name=f"o{q}")
             nc.scalar.copy(outs[q][:], back[q][:].rearrange("p (t j) -> p t j", t=4))
-            nc.sync.dma_start(out0_v[:, :, q * P : q * P + P], outs[q][:])
+            store(q)
 
-        def hand_on(q, engine_copy):
-            a = q * P
-            ob = keep.tile([P, P, 4], BF16, name=f"ob{q}", align_bytes=64)
-            interleave(engine_copy, ob[:], outs[q][:])
-            codes = keep.tile([P, P], I32, name=f"oc{q}", align_bytes=64)
-            nc.vector.quantize_mx(
-                out=codes[:].bitcast(FP8X4), scales=o_scales[:, a : a + P], in_=ob[:].rearrange("p n t -> p (n t)")
+        def along_cells(row, q):
+            return row[:, (q - 3) * P : (q - 2) * P].unsqueeze(1).to_broadcast([P, 4, P])
+
+        def kept_planes(q, kib):
+            kept[q] = placed([P, 4, P], F32, f"kept{q}", kib)
+            nc.gpsimd.tensor_tensor(kept[q][:], z[q], along_cells(keep_rate, q), MULT)
+
+        def moved_planes(q):
+            moved[q] = keep.tile([P, 4, P], F32, name=f"moved{q}")
+            nc.vector.tensor_tensor(
+                moved[q][:], eq[q][:].rearrange("p (t j) -> p t j", t=4), along_cells(rate, q), MULT
             )
-            nc.sync.dma_start(out1_v[:, a : a + P], codes[:])
 
-        z[0] = keep.tile([P, 4, 128], F32, name="z0")
-        z[1] = keep.tile([P, 4, 256], F32, name="z1")
-        gather(0, range(4))
-        gather(1, range(4))
-        nc.vector.tensor_scalar(keep_rate[:], rate[:], -1.0, 1.0, MULT, ADD)
+        def relax_planes(q):
+            outs[q] = keep.tile([P, 4, P], F32, name=f"o{q}")
+            nc.vector.tensor_tensor(outs[q][:], moved[q][:], kept[q][:], ADD)
+            store(q)
+
+        def round_out(q, engine_copy):
+            ob[q] = keep.tile([P, P, 4], BF16, name=f"ob{q}", align_bytes=64)
+            interleave(engine_copy, ob[q][:], outs[q][:])
+
+        def quant_out(q):
+            h, e = divmod(q, 2)
+            nc.vector.quantize_mx(
+                out=o_codes[h][:, P * e : P * e + P].bitcast(FP8X4),
+                scales=o_scales[:, P * q : P * q + P],
+                in_=ob[q][:].rearrange("p n t -> p (n t)"),
+            )
+            if q in (1, 2):
+                nc.sync.dma_start(out1_v[:, 256 * h : 256 * h + 256], o_codes[h][:])
+
+        gather(z01, 0, 256)
+        z[0], z[1] = z01[:, :, 0:P], z01[:, :, P : 2 * P]
+        z2 = placed([P, 4, P], F32, "z2", 26)
+        gather(z2, 256, P)
+        z[2] = z2[:]
         w2q = quant(w2g[:].rearrange("p t m j -> p (t m j)"), H, "w2q")
-        zb[0] = placed([P, 128, 4], BF16, "zb0", 2)
-        zb[1] = placed([P, 256, 4], BF16, "zb1", 3)
-        zb[2] = placed([P, 128, 4], BF16, "zb2", 11)
         turn_z(0)
         turn_z(1)
-        round_z(0, nc.scalar.copy)
-        quant_z(0)
-        product(0)
         turn_z(2)
-        round_z(1, nc.scalar.copy)
-        kept_share(0, 5)
-        z[2] = placed([P, 4, 128], F32, "z2", 1)
-        gather(2, range(4))
+        round_z(0, 14)
+        round_z(1, 15)
+        kept_turned(0, 18)
+        round_z(2, 46)
+        quant_z(0)
         quant_z(1)
-        product(1)
-        product(2)
-        relax(0)
-        turn(0)
-        round_z(2, nc.scalar.copy)
-        kept_share(1, 7)
-        kept_share(2, 9)
+        product_turned(0)
+        product_turned(1)
+        kept_turned(1, 20)
+        moved_turned(0)
+        z3 = placed([P, 4, P], F32, "z3", 32)
+        gather(z3, 384, P)
+        z[3] = z3[:]
+        round_z(3, 14)
+        kept_turned(2, 44)
         quant_z(2)
-        eq = psum.tile([P, 512], F32, name="acc")
-        for t in range(4):
-            nc.tensor.matmul_mx(
-                out=eq[:, P * t : P * t + P],
-                lhsT=w2q[0][:, P * t : P * t + P].bitcast(FP8X4),
-                lhsT_scale=w2q[1][:, P * t : P * t + P],
-                rhs=zq[2][0][:].bitcast(FP8X4),
-                rhs_scale=zq[2][1][:],
-                start=True,
-                stop=True,
-            )
+        turn_back_sum(0)
+        product_turned(2)
+        relax_turned(1)
+        turn_back(1)
         leave_psum(0)
-        relax(1)
-        relax(2)
-        turn(1)
-        turn(2)
-        kept = placed([P, 4, P], F32, "kept", 11)
-        nc.vector.tensor_tensor(kept[:], z[2][:], keep_rate[:, 0:P].unsqueeze(1).to_broadcast([P, 4, P]), MULT)
+        quant_z(3)
+        product_planes(3)
+        relax_turned(2)
+        turn_back(2)
+        kept_planes(3, 46)
+        round_out(0, nc.scalar.copy)
         leave_psum(1)
+        moved_planes(3)
+        quant_out(0)
         leave_psum(2)
-        moved = keep.tile([P, 4, P], F32, name="moved")
-        nc.vector.tensor_tensor(
-            moved[:], eq[:].rearrange("p (t j) -> p t j", t=4), rate[:, 0:P].unsqueeze(1).to_broadcast([P, 4, P]), MULT
-        )
-        outs[3] = keep.tile([P, 4, P], F32, name="o3")
-        nc.vector.tensor_tensor(outs[3][:], moved[:], kept[:], ADD)
-        nc.sync.dma_start(out0_v[:, :, 3 * P : 4 * P], outs[3][:])
-        hand_on(0, nc.scalar.copy)
-        hand_on(1, nc.scalar.copy)
-        hand_on(3, nc.vector.tensor_copy)
-        hand_on(2, nc.vector.tensor_copy)
+        round_out(1, nc.scalar.copy)
+        relax_planes(3)
+        round_out(2, nc.vector.tensor_copy)
+        round_out(3, nc.vector.tensor_copy)
+        quant_out(1)
+        quant_out(3)
+        quant_out(2)
         for q in range(4):
             (nc.scalar, nc.sync)[q % 2].dma_start(
                 out_2[0, q:16:4, :].bitcast(I32), o_scales[q:P:32, :].bitcast(I32)

@@ -80,7 +80,7 @@ def tile_picked_lbm8_none_po_kernel(
         ]
 
         w2_rows = w2.rearrange("(p j) c -> p j c", j=4)
-        w2_cuts = ((0, 256, 22), (256, 64, 26), (320, 192, 28))
+        w2_cuts = ((0, 128, 22), (128, 64, 26), (192, 320, 56))
         w2_raw = [placed([P, 4, n], F32, f"w2_raw{h}", kib) for h, (a, n, kib) in enumerate(w2_cuts)]
         for h, (a, n, kib) in enumerate(w2_cuts):
             nc.sync.dma_start(w2_raw[h][:], w2_rows[:, :, a : a + n])

@@ -25,17 +25,23 @@ def tile_picked_lbm8_none_po_kernel(
     nc = tc.nc
     with ExitStack() as ctx:
         keep = ctx.enter_context(tc.tile_pool(name="keep", bufs=1))
-        shared = ctx.enter_context(tc.tile_pool(name="shared", bufs=1))
+        queue = ctx.enter_context(tc.tile_pool(name="queue", bufs=1))
         psum = ctx.enter_context(tc.psum_pool(name="psum", bufs=8))
 
-        def placed(shape, dtype, name, kib):
-            return shared.tile(shape, dtype, name=name, offset=1024 * kib, align_bytes=64)
+        def on_vector(shape, dtype, name):
+            return queue.tile(shape, dtype, name=name, tag="vector", bufs=26, align_bytes=64)
+
+        def on_scalar(shape, dtype, name):
+            return queue.tile(shape, dtype, name=name, tag="scalar", bufs=16, align_bytes=64)
+
+        def on_gpsimd(shape, dtype, name):
+            return queue.tile(shape, dtype, name=name, tag="gpsimd", bufs=4, align_bytes=64)
 
         offs_t = keep.tile([P, S // 16], U16, name="offs_t")
         stream_t = keep.tile([P, S // 16], U16, name="stream_t")
-        xw = placed([P, T], I32, "xw", 36)
-        xs = placed([P, T], U8, "xs", 0)
-        w1_raw = placed([P, 4, H], F32, "w1_raw", 2)
+        xw = keep.tile([P, T], I32, name="xw")
+        xs = keep.tile([P, T], U8, name="xs")
+        w1_raw = keep.tile([P, 4, H], F32, name="w1_raw")
         ident = keep.tile([P, P], F32, name="ident")
 
         nc.vector.memset(xs[:].bitcast(I32), 0)
@@ -47,26 +53,22 @@ def tile_picked_lbm8_none_po_kernel(
         nc.sync.dma_start(stream_t[:], stream)
         make_identity(nc, ident[:])
 
-        xg_s = keep.tile([P, S], U8, name="xg_s", align_bytes=64)
-        nc.vector.tensor_copy(xg_s[:], xs[:].indirect(offs_t[:]))
-
         def scalar_copy(dst, src):
             nc.scalar.activation(dst, src, COPY)
 
         def gpsimd_copy(dst, src):
             nc.gpsimd.tensor_scalar(dst, src, 1.0, 0.0, MULT, ADD)
 
-        def deal(engine_copy, u):
-            grouped = placed([P, 2, P, 4], BF16, f"w1g{u}", 10 + 2 * u)
+        def deal(engine_copy, make, u):
+            grouped = make([P, 2, P, 4], BF16, f"w1g{u}")
             engine_copy(
                 grouped[:].rearrange("p t m j -> p m j t"),
                 w1_raw[:].rearrange("p j (m t) -> p m j t", t=4)[:, :, :, 2 * u : 2 * u + 2],
             )
             return grouped
 
-        def quant(grouped_flat, width, name, codes=None):
-            if codes is None:
-                codes = keep.tile([P, width], U32, name=name + "_c", align_bytes=64)
+        def quant(grouped_flat, width, name):
+            codes = on_vector([P, width], U32, name + "_c")
             scales = keep.tile([P, width], U8, name=name + "_s", align_bytes=64)
             nc.vector.quantize_mx(out=codes[:].bitcast(FP8X4), scales=scales[:], in_=grouped_flat)
             return codes, scales
@@ -74,31 +76,35 @@ def tile_picked_lbm8_none_po_kernel(
         def interleave(engine_copy, dst, src):
             engine_copy(dst.rearrange("p (c i) t -> p c t i", i=4), src.rearrange("p t (c i) -> p c t i", i=4))
 
-        w1g = [deal(nc.vector.tensor_copy, 0), deal(scalar_copy, 1)]
-        w1q = [
-            quant(w1g[0][:].rearrange("p t m j -> p (t m j)"), 256, "w1q0", placed([P, 256], U32, "w1q0_c", 0)),
-        ]
+        w1g = [deal(nc.vector.tensor_copy, on_vector, 0), deal(scalar_copy, on_scalar, 1)]
+        xg_s = on_vector([P, S], U8, "xg_s")
+        nc.vector.tensor_copy(xg_s[:], xs[:].indirect(offs_t[:]))
+        w1q = [quant(w1g[0][:].rearrange("p t m j -> p (t m j)"), 256, "w1q0")]
 
         w2_rows = w2.rearrange("(p j) c -> p j c", j=4)
-        w2_cuts = ((0, 128, 22), (128, 64, 26), (192, 320, 56))
-        w2_raw = [placed([P, 4, n], F32, f"w2_raw{h}", kib) for h, (a, n, kib) in enumerate(w2_cuts)]
-        for h, (a, n, kib) in enumerate(w2_cuts):
+        w2_cuts = ((0, 128), (128, 64), (192, 320))
+        w2_raw = [keep.tile([P, 4, n], F32, name=f"w2_raw{h}") for h, (a, n) in enumerate(w2_cuts)]
+        for h in range(3):
+            a, n = w2_cuts[h]
             nc.sync.dma_start(w2_raw[h][:], w2_rows[:, :, a : a + n])
 
-        rate = keep.tile([P, 128 + 3], F32, name="rate")
-        nc.sync.dma_start(rate[:, 0:128], om[:, 384:512])
+        NT = 1
+        NP = S - P * NT
+        rate = keep.tile([P, NP + NT], F32, name="rate")
+        nc.sync.dma_start(rate[:, 0:NP], om[:, P * NT : S])
         with nc.allow_non_contiguous_dma(reason="one rate for each partition"):
-            nc.sync.dma_start(rate[:, 128:131], om[0, 0:384].rearrange("(q p) -> p q", p=P))
+            nc.sync.dma_start(rate[:, NP : NP + NT], om[0, 0 : P * NT].rearrange("(q p) -> p q", p=P))
 
-        xg = [keep.tile([P, 256], U32, name="xg0", align_bytes=64), keep.tile([P, 256], U32, name="xg1", align_bytes=64)]
+        xg = []
         for h in range(2):
+            xg.append(on_vector([P, 256], U32, f"xg{h}"))
             nc.vector.tensor_copy(xg[h][:], xw[:].bitcast(U32).indirect(offs_t[:, 16 * h : 16 * h + 16]))
 
-        w1q.append(quant(w1g[1][:].rearrange("p t m j -> p (t m j)"), 256, "w1q1", placed([P, 256], U32, "w1q1_c", 36)))
-        w2g = placed([P, 4, P, 4], BF16, "w2g", 32)
+        w1q.append(quant(w1g[1][:].rearrange("p t m j -> p (t m j)"), 256, "w1q1"))
+        w2g = on_vector([P, 4, P, 4], BF16, "w2g")
 
         def deal_w2(engine_copy, h, walk):
-            a, n, kib = w2_cuts[h]
+            a, n = w2_cuts[h]
             engine_copy(
                 w2g[:, :, a // 4 : (a + n) // 4, :].rearrange("p t m j -> " + walk),
                 w2_raw[h][:].rearrange("p j (m t) -> " + walk, t=4),
@@ -106,7 +112,7 @@ def tile_picked_lbm8_none_po_kernel(
 
         deal_w2(nc.vector.tensor_copy, 0, "p m j t")
 
-        y = [keep.tile([P, S], F32, name=f"y{t}") for t in range(4)]
+        y = [on_scalar([P, S], F32, f"y{t}") for t in range(4)]
         for t, h in ((0, 0), (1, 0), (0, 1), (1, 1), (2, 0), (2, 1), (3, 0), (3, 1)):
             u, e = divmod(t, 2)
             if t < 2 or h == 0:
@@ -127,24 +133,28 @@ def tile_picked_lbm8_none_po_kernel(
 
         deal_w2(nc.scalar.copy, 1, "p m j t")
         deal_w2(gpsimd_copy, 2, "p t m j")
-        keep_rate = keep.tile([P, 128 + 3], F32, name="keep_rate")
+        keep_rate = on_gpsimd([P, NP + NT], F32, "keep_rate")
         nc.gpsimd.tensor_scalar(keep_rate[:], rate[:], -1.0, 1.0, MULT, ADD)
 
         o_scales = keep.tile([P, S], U8, name="o_scales", align_bytes=64)
-        o_codes = [keep.tile([P, 256], I32, name=f"o_codes{h}", align_bytes=64) for h in range(2)]
         out0_v = out_0.rearrange("(p t) j -> p t j", t=4)
         out1_v = out_1[0].rearrange("p n t -> p (n t)").bitcast(I32)
 
-        z01 = placed([P, 4, 256], F32, "z01", 22)
-        z, zb, zq, z_t, u_t, eq, o_t, back, outs, kept, moved, ob = ({} for i in range(12))
+        z, zb, zq, z_t, u_t, eq, o_t, back, outs, kept, moved, ob, o_codes, w2q = ({} for i in range(14))
 
-        def gather(dst, a, n):
+        def gather(first, count):
+            dst = on_vector([P, 4, P * count], F32, f"z{first}")
             for t in range(4):
-                nc.vector.tensor_copy(dst[:, t, :], y[t][:].indirect(stream_t[:, a // 16 : (a + n) // 16]))
+                nc.vector.tensor_copy(dst[:, t, :], y[t][:].indirect(stream_t[:, 8 * first : 8 * (first + count)]))
+            for q in range(count):
+                z[first + q] = dst[:, :, P * q : P * q + P]
 
-        def round_z(q, kib):
-            zb[q] = placed([P, P, 4], BF16, f"zb{q}", kib)
-            interleave(nc.scalar.copy, zb[q][:], z[q])
+        def quant_w2():
+            w2q[0], w2q[1] = quant(w2g[:].rearrange("p t m j -> p (t m j)"), H, "w2q")
+
+        def round_z(q, engine_copy=nc.scalar.copy, make=on_scalar):
+            zb[q] = make([P, P, 4], BF16, f"zb{q}")
+            interleave(engine_copy, zb[q][:], z[q])
 
         def quant_z(q):
             zq[q] = quant(zb[q][:].rearrange("p n t -> p (n t)"), P, f"zq{q}")
@@ -154,9 +164,9 @@ def tile_picked_lbm8_none_po_kernel(
             for t in range(4):
                 nc.tensor.transpose(z_t[q][:, P * t : P * t + P], z[q][:, t, :], ident[:])
 
-        def kept_turned(q, kib):
-            u_t[q] = placed([P, 512], F32, f"u_t{q}", kib)
-            nc.scalar.activation(u_t[q][:], z_t[q][:], COPY, scale=keep_rate[:, 128 + q : 129 + q])
+        def kept_turned(q):
+            u_t[q] = on_scalar([P, 512], F32, f"u_t{q}")
+            nc.scalar.activation(u_t[q][:], z_t[q][:], COPY, scale=keep_rate[:, NP + q : NP + q + 1])
 
         def product_turned(q):
             eq[q] = psum.tile([P, 512], F32, name="acc")
@@ -184,120 +194,120 @@ def tile_picked_lbm8_none_po_kernel(
                 )
 
         def relax_turned(q):
-            o_t[q] = keep.tile([P, 4, P], F32, name=f"o_t{q}")
-            nc.vector.scalar_tensor_tensor(
-                o_t[q][:].rearrange("p t m -> p (t m)"), eq[q][:], rate[:, 128 + q : 129 + q], u_t[q][:], MULT, ADD
-            )
+            o_t[q] = on_vector([P, 512], F32, f"o_t{q}")
+            nc.vector.scalar_tensor_tensor(o_t[q][:], eq[q][:], rate[:, NP + q : NP + q + 1], u_t[q][:], MULT, ADD)
 
         def moved_turned(q):
-            o_t[q] = keep.tile([P, 512], F32, name=f"e_t{q}")
-            nc.scalar.activation(o_t[q][:], eq[q][:], COPY, scale=rate[:, 128 + q : 129 + q])
+            o_t[q] = on_scalar([P, 512], F32, f"e_t{q}")
+            nc.scalar.activation(o_t[q][:], eq[q][:], COPY, scale=rate[:, NP + q : NP + q + 1])
 
-        def turn_back_sum(q):
-            back[q] = psum.tile([P, 512], F32, name="acc")
+        def turn_parts(q, parts, start, stop):
+            if start:
+                back[q] = psum.tile([P, 512], F32, name="acc")
             for t in range(4):
-                for first, part in ((True, u_t[q]), (False, o_t[q])):
+                for n, part in enumerate(parts):
                     nc.tensor.matmul(
                         back[q][:, P * t : P * t + P],
                         part[:, P * t : P * t + P],
                         ident[:],
-                        start=first,
-                        stop=not first,
+                        start=start and n == 0 and (t == 0 or stop),
+                        stop=stop and n == len(parts) - 1 and (t == 3 or start),
                         is_transpose=True,
                     )
 
+        def turn_back_sum(q):
+            turn_parts(q, (u_t[q], o_t[q]), True, True)
+
+        def turn_kept(q):
+            turn_parts(q, (u_t[q],), True, False)
+
+        def turn_moved(q):
+            turn_parts(q, (o_t[q],), False, True)
+
         def turn_back(q):
-            back[q] = psum.tile([P, 512], F32, name="acc")
-            for t in range(4):
-                nc.tensor.transpose(back[q][:, P * t : P * t + P], o_t[q][:, t, :], ident[:])
+            turn_parts(q, (o_t[q],), True, True)
 
         def store(q):
             nc.sync.dma_start(out0_v[:, :, q * P : q * P + P], outs[q][:])
 
         def leave_psum(q):
-            outs[q] = keep.tile([P, 4, P], F32, name=f"o{q}")
+            outs[q] = on_scalar([P, 4, P], F32, f"o{q}")
             nc.scalar.copy(outs[q][:], back[q][:].rearrange("p (t j) -> p t j", t=4))
             store(q)
 
         def along_cells(row, q):
-            return row[:, (q - 3) * P : (q - 2) * P].unsqueeze(1).to_broadcast([P, 4, P])
+            first = (q - NT) * P
+            return row[:, first : first + P].unsqueeze(1).to_broadcast([P, 4, P])
 
-        def kept_planes(q, kib):
-            kept[q] = placed([P, 4, P], F32, f"kept{q}", kib)
+        def kept_planes(q):
+            kept[q] = on_gpsimd([P, 4, P], F32, f"kept{q}")
             nc.gpsimd.tensor_tensor(kept[q][:], z[q], along_cells(keep_rate, q), MULT)
 
         def moved_planes(q):
-            moved[q] = keep.tile([P, 4, P], F32, name=f"moved{q}")
+            moved[q] = on_vector([P, 4, P], F32, f"moved{q}")
             nc.vector.tensor_tensor(
                 moved[q][:], eq[q][:].rearrange("p (t j) -> p t j", t=4), along_cells(rate, q), MULT
             )
 
         def relax_planes(q):
-            outs[q] = keep.tile([P, 4, P], F32, name=f"o{q}")
+            outs[q] = on_vector([P, 4, P], F32, f"o{q}")
             nc.vector.tensor_tensor(outs[q][:], moved[q][:], kept[q][:], ADD)
             store(q)
 
-        def round_out(q, engine_copy):
-            ob[q] = keep.tile([P, P, 4], BF16, name=f"ob{q}", align_bytes=64)
+        def round_out(q, engine_copy=nc.scalar.copy, make=on_scalar):
+            ob[q] = make([P, P, 4], BF16, f"ob{q}")
             interleave(engine_copy, ob[q][:], outs[q][:])
 
-        def quant_out(q):
+        def quant_out(q, first, last):
             h, e = divmod(q, 2)
+            if first:
+                o_codes[h] = on_vector([P, 256], I32, f"o_codes{h}")
             nc.vector.quantize_mx(
                 out=o_codes[h][:, P * e : P * e + P].bitcast(FP8X4),
                 scales=o_scales[:, P * q : P * q + P],
                 in_=ob[q][:].rearrange("p n t -> p (n t)"),
             )
-            if q in (1, 2):
+            if last:
                 nc.sync.dma_start(out1_v[:, 256 * h : 256 * h + 256], o_codes[h][:])
 
-        gather(z01, 0, 256)
-        z[0], z[1] = z01[:, :, 0:P], z01[:, :, P : 2 * P]
-        z2 = placed([P, 4, P], F32, "z2", 26)
-        gather(z2, 256, P)
-        z[2] = z2[:]
-        w2q = quant(w2g[:].rearrange("p t m j -> p (t m j)"), H, "w2q")
+        gather(0, 2)
+        quant_w2()
         turn_z(0)
-        turn_z(1)
-        turn_z(2)
-        round_z(0, 14)
-        round_z(1, 15)
-        kept_turned(0, 18)
-        round_z(2, 46)
+        round_z(0)
+        round_z(1)
+        gather(2, 1)
+        kept_planes(1)
         quant_z(0)
         quant_z(1)
+        kept_turned(0)
+        round_z(2)
         product_turned(0)
-        product_turned(1)
-        kept_turned(1, 20)
-        moved_turned(0)
-        z3 = placed([P, 4, P], F32, "z3", 32)
-        gather(z3, 384, P)
-        z[3] = z3[:]
-        round_z(3, 14)
-        kept_turned(2, 44)
+        product_planes(1)
+        gather(3, 1)
+        kept_planes(2)
         quant_z(2)
-        turn_back_sum(0)
-        product_turned(2)
-        relax_turned(1)
-        turn_back(1)
-        leave_psum(0)
+        round_z(3)
+        relax_turned(0)
+        product_planes(2)
+        moved_planes(1)
+        turn_back(0)
         quant_z(3)
+        kept_planes(3)
         product_planes(3)
-        relax_turned(2)
-        turn_back(2)
-        kept_planes(3, 46)
-        round_out(0, nc.scalar.copy)
-        leave_psum(1)
+        relax_planes(1)
+        moved_planes(2)
+        leave_psum(0)
         moved_planes(3)
-        quant_out(0)
-        leave_psum(2)
-        round_out(1, nc.scalar.copy)
+        round_out(0)
+        round_out(1)
+        relax_planes(2)
         relax_planes(3)
-        round_out(2, nc.vector.tensor_copy)
-        round_out(3, nc.vector.tensor_copy)
-        quant_out(1)
-        quant_out(3)
-        quant_out(2)
+        round_out(2)
+        round_out(3)
+        quant_out(0, True, False)
+        quant_out(1, False, True)
+        quant_out(2, True, False)
+        quant_out(3, False, True)
         for q in range(4):
             (nc.scalar, nc.sync)[q % 2].dma_start(
                 out_2[0, q:16:4, :].bitcast(I32), o_scales[q:P:32, :].bitcast(I32)

@@ -26,6 +26,7 @@ def tile_picked_lbm8_none_po_kernel(
     with ExitStack() as ctx:
         keep = ctx.enter_context(tc.tile_pool(name="keep", bufs=1))
         queue = ctx.enter_context(tc.tile_pool(name="queue", bufs=1))
+        shared = ctx.enter_context(tc.tile_pool(name="shared", bufs=1))
         psum = ctx.enter_context(tc.psum_pool(name="psum", bufs=8))
 
         def on_vector(shape, dtype, name):
@@ -36,6 +37,9 @@ def tile_picked_lbm8_none_po_kernel(
 
         def on_gpsimd(shape, dtype, name):
             return queue.tile(shape, dtype, name=name, tag="gpsimd", bufs=4, align_bytes=64)
+
+        def placed(shape, dtype, name, kib):
+            return shared.tile(shape, dtype, name=name, offset=1024 * kib, align_bytes=64)
 
         offs_t = keep.tile([P, S // 16], U16, name="offs_t")
         stream_t = keep.tile([P, S // 16], U16, name="stream_t")
@@ -82,8 +86,8 @@ def tile_picked_lbm8_none_po_kernel(
         w1q = [quant(w1g[0][:].rearrange("p t m j -> p (t m j)"), 256, "w1q0")]
 
         w2_rows = w2.rearrange("(p j) c -> p j c", j=4)
-        w2_cuts = ((0, 128), (128, 64), (192, 320))
-        w2_raw = [keep.tile([P, 4, n], F32, name=f"w2_raw{h}") for h, (a, n) in enumerate(w2_cuts)]
+        w2_cuts = ((0, 192), (192, 128), (320, 192))
+        w2_raw = [placed([P, 4, n], F32, f"w2_raw{h}", 16 + 8 * h) for h, (a, n) in enumerate(w2_cuts)]
         for h in range(3):
             a, n = w2_cuts[h]
             nc.sync.dma_start(w2_raw[h][:], w2_rows[:, :, a : a + n])
@@ -101,7 +105,7 @@ def tile_picked_lbm8_none_po_kernel(
             nc.vector.tensor_copy(xg[h][:], xw[:].bitcast(U32).indirect(offs_t[:, 16 * h : 16 * h + 16]))
 
         w1q.append(quant(w1g[1][:].rearrange("p t m j -> p (t m j)"), 256, "w1q1"))
-        w2g = on_vector([P, 4, P, 4], BF16, "w2g")
+        w2g = placed([P, 4, P, 4], BF16, "w2g", 0)
 
         def deal_w2(engine_copy, h, walk):
             a, n = w2_cuts[h]
@@ -131,8 +135,8 @@ def tile_picked_lbm8_none_po_kernel(
             elif h == 1:
                 nc.scalar.copy(y[t][:], acc[:])
 
-        deal_w2(nc.scalar.copy, 1, "p m j t")
-        deal_w2(gpsimd_copy, 2, "p t m j")
+        deal_w2(gpsimd_copy, 1, "p t m j")
+        deal_w2(nc.scalar.copy, 2, "p m j t")
         keep_rate = on_gpsimd([P, NP + NT], F32, "keep_rate")
         nc.gpsimd.tensor_scalar(keep_rate[:], rate[:], -1.0, 1.0, MULT, ADD)
 
@@ -143,21 +147,54 @@ def tile_picked_lbm8_none_po_kernel(
         z, zb, zq, z_t, u_t, eq, o_t, back, outs, kept, moved, ob, o_codes, w2q = ({} for i in range(14))
 
         def gather(first, count):
-            dst = on_vector([P, 4, P * count], F32, f"z{first}")
+            if first == 0:
+                dst = placed([P, 4, P * count], F32, "z0", 16)
+            else:
+                dst = on_vector([P, 4, P * count], F32, f"z{first}")
             for t in range(4):
                 nc.vector.tensor_copy(dst[:, t, :], y[t][:].indirect(stream_t[:, 8 * first : 8 * (first + count)]))
+            if first == 0:
+                z["pair"] = dst[:]
             for q in range(count):
                 z[first + q] = dst[:, :, P * q : P * q + P]
 
         def quant_w2():
             w2q[0], w2q[1] = quant(w2g[:].rearrange("p t m j -> p (t m j)"), H, "w2q")
 
-        def round_z(q, engine_copy=nc.scalar.copy, make=on_scalar):
-            zb[q] = make([P, P, 4], BF16, f"zb{q}")
+        def round_z(q, engine_copy=nc.scalar.copy):
+            zb[q] = on_scalar([P, P, 4], BF16, f"zb{q}")
             interleave(engine_copy, zb[q][:], z[q])
 
         def quant_z(q):
-            zq[q] = quant(zb[q][:].rearrange("p n t -> p (n t)"), P, f"zq{q}")
+            codes, scales = quant(zb[q][:].rearrange("p n t -> p (n t)"), P, f"zq{q}")
+            zq[q] = (codes[:], scales[:])
+
+        def round_z_pair():
+            zb[0] = on_scalar([P, 2 * P, 4], BF16, "zb01")
+            interleave(nc.scalar.copy, zb[0][:], z["pair"])
+
+        def quant_z_pair():
+            codes, scales = quant(zb[0][:].rearrange("p n t -> p (n t)"), 2 * P, "zq01")
+            for q in range(2):
+                zq[q] = (codes[:, P * q : P * q + P], scales[:, P * q : P * q + P])
+
+        def round_out_pair(q):
+            if "pair" not in ob:
+                ob["pair"] = on_scalar([P, 2 * P, 4], BF16, "ob01")
+            interleave(nc.scalar.copy, ob["pair"][:, P * q : P * q + P, :], outs[q][:])
+
+        def quant_out_pair():
+            o_codes[0] = on_vector([P, 256], I32, "o_codes0")
+            nc.vector.quantize_mx(
+                out=o_codes[0][:].bitcast(FP8X4),
+                scales=o_scales[:, 0 : 2 * P],
+                in_=ob["pair"][:].rearrange("p n t -> p (n t)"),
+            )
+            nc.sync.dma_start(out1_v[:, 0:256], o_codes[0][:])
+
+        def kept_free(q):
+            kept[q] = on_gpsimd([P, 4, P], F32, f"kept{q}")
+            nc.gpsimd.tensor_tensor(kept[q][:], z[q], along_cells(keep_rate, q), MULT)
 
         def turn_z(q):
             z_t[q] = psum.tile([P, 512], F32, name="acc")
@@ -172,8 +209,8 @@ def tile_picked_lbm8_none_po_kernel(
             eq[q] = psum.tile([P, 512], F32, name="acc")
             nc.tensor.matmul_mx(
                 out=eq[q][:],
-                lhsT=zq[q][0][:].bitcast(FP8X4),
-                lhsT_scale=zq[q][1][:],
+                lhsT=zq[q][0].bitcast(FP8X4),
+                lhsT_scale=zq[q][1],
                 rhs=w2q[0][:].bitcast(FP8X4),
                 rhs_scale=w2q[1][:],
                 start=True,
@@ -187,8 +224,8 @@ def tile_picked_lbm8_none_po_kernel(
                     out=eq[q][:, P * t : P * t + P],
                     lhsT=w2q[0][:, P * t : P * t + P].bitcast(FP8X4),
                     lhsT_scale=w2q[1][:, P * t : P * t + P],
-                    rhs=zq[q][0][:].bitcast(FP8X4),
-                    rhs_scale=zq[q][1][:],
+                    rhs=zq[q][0].bitcast(FP8X4),
+                    rhs_scale=zq[q][1],
                     start=True,
                     stop=True,
                 )
@@ -239,9 +276,18 @@ def tile_picked_lbm8_none_po_kernel(
             first = (q - NT) * P
             return row[:, first : first + P].unsqueeze(1).to_broadcast([P, 4, P])
 
-        def kept_planes(q):
-            kept[q] = on_gpsimd([P, 4, P], F32, f"kept{q}")
+        def kept_planes(q, kib):
+            kept[q] = placed([P, 4, P], F32, f"kept{q}", kib)
             nc.gpsimd.tensor_tensor(kept[q][:], z[q], along_cells(keep_rate, q), MULT)
+
+        def kept_planes_vector(q):
+            kept[q] = on_vector([P, 4, P], F32, f"kept{q}")
+            nc.vector.tensor_tensor(kept[q][:], z[q], along_cells(keep_rate, q), MULT)
+
+        def relax_back(q):
+            outs[q] = on_vector([P, 4, P], F32, f"o{q}")
+            nc.vector.tensor_tensor(outs[q][:], back[q][:].rearrange("p (t j) -> p t j", t=4), kept[q][:], ADD)
+            store(q)
 
         def moved_planes(q):
             moved[q] = on_vector([P, 4, P], F32, f"moved{q}")
@@ -273,18 +319,16 @@ def tile_picked_lbm8_none_po_kernel(
         gather(0, 2)
         quant_w2()
         turn_z(0)
-        round_z(0)
-        round_z(1)
+        round_z_pair()
         gather(2, 1)
-        kept_planes(1)
-        quant_z(0)
-        quant_z(1)
+        kept_planes(1, 32)
+        quant_z_pair()
         kept_turned(0)
         round_z(2)
         product_turned(0)
         product_planes(1)
         gather(3, 1)
-        kept_planes(2)
+        kept_free(2)
         quant_z(2)
         round_z(3)
         relax_turned(0)
@@ -292,20 +336,19 @@ def tile_picked_lbm8_none_po_kernel(
         moved_planes(1)
         turn_back(0)
         quant_z(3)
-        kept_planes(3)
+        kept_free(3)
         product_planes(3)
         relax_planes(1)
         moved_planes(2)
         leave_psum(0)
         moved_planes(3)
-        round_out(0)
-        round_out(1)
+        round_out_pair(0)
+        round_out_pair(1)
         relax_planes(2)
         relax_planes(3)
         round_out(2)
-        round_out(3)
-        quant_out(0, True, False)
-        quant_out(1, False, True)
+        quant_out_pair()
+        round_out(3, nc.vector.tensor_copy, on_vector)
         quant_out(2, True, False)
         quant_out(3, False, True)
         for q in range(4):

@@ -33,7 +33,7 @@ def tile_picked_lbm8_none_po_kernel(
             return queue.tile(shape, dtype, name=name, tag="vector", bufs=26, align_bytes=64)
 
         def on_scalar(shape, dtype, name):
-            return queue.tile(shape, dtype, name=name, tag="scalar", bufs=16, align_bytes=64)
+            return queue.tile(shape, dtype, name=name, tag="scalar", bufs=20, align_bytes=64)
 
         def on_gpsimd(shape, dtype, name):
             return queue.tile(shape, dtype, name=name, tag="gpsimd", bufs=4, align_bytes=64)
@@ -86,7 +86,7 @@ def tile_picked_lbm8_none_po_kernel(
         w1q = [quant(w1g[0][:].rearrange("p t m j -> p (t m j)"), 256, "w1q0")]
 
         w2_rows = w2.rearrange("(p j) c -> p j c", j=4)
-        w2_cuts = ((0, 192), (192, 128), (320, 192))
+        w2_cuts = ((0, 128), (128, 256), (384, 128))
         w2_raw = [placed([P, 4, n], F32, f"w2_raw{h}", 16 + 8 * h) for h, (a, n) in enumerate(w2_cuts)]
         for h in range(3):
             a, n = w2_cuts[h]
@@ -137,8 +137,8 @@ def tile_picked_lbm8_none_po_kernel(
 
         deal_w2(gpsimd_copy, 1, "p t m j")
         deal_w2(nc.scalar.copy, 2, "p m j t")
-        keep_rate = on_gpsimd([P, NP + NT], F32, "keep_rate")
-        nc.gpsimd.tensor_scalar(keep_rate[:], rate[:], -1.0, 1.0, MULT, ADD)
+        keep_rate = on_scalar([P, NP + NT], F32, "keep_rate")
+        nc.scalar.activation(keep_rate[:], rate[:], COPY, scale=-1.0, bias=1.0)
 
         o_scales = keep.tile([P, S], U8, name="o_scales", align_bytes=64)
         out0_v = out_0.rearrange("(p t) j -> p t j", t=4)
@@ -158,11 +158,21 @@ def tile_picked_lbm8_none_po_kernel(
             for q in range(count):
                 z[first + q] = dst[:, :, P * q : P * q + P]
 
+        def gather_two():
+            dst = [placed([P, 4, P], F32, "z0", 16), on_vector([P, 4, P], F32, "z1")]
+            for t in range(4):
+                for q in range(2):
+                    nc.vector.tensor_copy(dst[q][:, t, :], y[t][:].indirect(stream_t[:, 8 * q : 8 * q + 8]))
+            z[0], z[1] = dst[0][:], dst[1][:]
+
         def quant_w2():
             w2q[0], w2q[1] = quant(w2g[:].rearrange("p t m j -> p (t m j)"), H, "w2q")
 
         def round_z(q, engine_copy=nc.scalar.copy):
-            zb[q] = on_scalar([P, P, 4], BF16, f"zb{q}")
+            if q == 3:
+                zb[q] = placed([P, P, 4], BF16, "zb3", 8)
+            else:
+                zb[q] = on_scalar([P, P, 4], BF16, f"zb{q}")
             interleave(engine_copy, zb[q][:], z[q])
 
         def quant_z(q):
@@ -321,7 +331,7 @@ def tile_picked_lbm8_none_po_kernel(
         turn_z(0)
         round_z_pair()
         gather(2, 1)
-        kept_planes(1, 32)
+        kept_free(1)
         quant_z_pair()
         kept_turned(0)
         round_z(2)
@@ -336,14 +346,14 @@ def tile_picked_lbm8_none_po_kernel(
         moved_planes(1)
         turn_back(0)
         quant_z(3)
-        kept_free(3)
+        kept_planes(3, 8)
         product_planes(3)
         relax_planes(1)
         moved_planes(2)
         leave_psum(0)
         moved_planes(3)
-        round_out_pair(0)
         round_out_pair(1)
+        round_out_pair(0)
         relax_planes(2)
         relax_planes(3)
         round_out(2)

@@ -81,9 +81,9 @@ def tile_picked_lbm8_none_po_kernel(
             engine_copy(dst.rearrange("p (c i) t -> p c t i", i=4), src.rearrange("p t (c i) -> p c t i", i=4))
 
         w1g = [deal(nc.vector.tensor_copy, on_vector, 0), deal(scalar_copy, on_scalar, 1)]
+        w1q = [quant(w1g[0][:].rearrange("p t m j -> p (t m j)"), 256, "w1q0")]
         xg_s = on_vector([P, S], U8, "xg_s")
         nc.vector.tensor_copy(xg_s[:], xs[:].indirect(offs_t[:]))
-        w1q = [quant(w1g[0][:].rearrange("p t m j -> p (t m j)"), 256, "w1q0")]
 
         w2_rows = w2.rearrange("(p j) c -> p j c", j=4)
         w2_cuts = ((0, 128), (128, 256), (384, 128))
@@ -314,6 +314,11 @@ def tile_picked_lbm8_none_po_kernel(
             ob[q] = make([P, P, 4], BF16, f"ob{q}")
             interleave(engine_copy, ob[q][:], outs[q][:])
 
+        def round_out_shared(q):
+            ob[q] = on_vector([P, P, 4], BF16, f"ob{q}")
+            interleave(nc.vector.tensor_copy, ob[q][:, 64:P, :], outs[q][:, :, 64:P])
+            interleave(nc.scalar.copy, ob[q][:, 0:64, :], outs[q][:, :, 0:64])
+
         def quant_out(q, first, last):
             h, e = divmod(q, 2)
             if first:
@@ -358,7 +363,7 @@ def tile_picked_lbm8_none_po_kernel(
         relax_planes(3)
         round_out(2)
         quant_out_pair()
-        round_out(3, nc.vector.tensor_copy, on_vector)
+        round_out_shared(3)
         quant_out(2, True, False)
         quant_out(3, False, True)
         for q in range(4):

@@ -12,11 +12,12 @@ U8 = mybir.dt.uint8
 FP8X4 = mybir.dt.float8_e4m3fn_x4
 MULT = mybir.AluOpType.mult
 ADD = mybir.AluOpType.add
+COPY = mybir.ActivationFunctionType.Copy
 
 P = 128
 K, T, S, H = 512, 2048, 512, 512
 FLOPS = 2 * 2 * 512 * 512 * 512
-COPY = mybir.ActivationFunctionType.Copy
+TURNED = 2
 
 
 def tile_picked_lbm8_none_po_kernel(
@@ -87,17 +88,16 @@ def tile_picked_lbm8_none_po_kernel(
 
         w2_rows = w2.rearrange("(p j) c -> p j c", j=4)
         w2_cuts = ((0, 128), (128, 256), (384, 128))
-        w2_raw = [placed([P, 4, n], F32, f"w2_raw{h}", 16 + 8 * h) for h, (a, n) in enumerate(w2_cuts)]
+        w2_raw = [keep.tile([P, 4, n], F32, name=f"w2_raw{h}") for h, (a, n) in enumerate(w2_cuts)]
         for h in range(3):
             a, n = w2_cuts[h]
             nc.sync.dma_start(w2_raw[h][:], w2_rows[:, :, a : a + n])
 
-        NT = 1
-        NP = S - P * NT
-        rate = keep.tile([P, NP + NT], F32, name="rate")
-        nc.sync.dma_start(rate[:, 0:NP], om[:, P * NT : S])
+        NP = S - P * TURNED
+        rate = keep.tile([P, NP + TURNED], F32, name="rate")
+        nc.sync.dma_start(rate[:, 0:NP], om[:, P * TURNED : S])
         with nc.allow_non_contiguous_dma(reason="one rate for each partition"):
-            nc.sync.dma_start(rate[:, NP : NP + NT], om[0, 0 : P * NT].rearrange("(q p) -> p q", p=P))
+            nc.sync.dma_start(rate[:, NP : NP + TURNED], om[0, 0 : P * TURNED].rearrange("(q p) -> p q", p=P))
 
         xg = []
         for h in range(2):
@@ -105,7 +105,7 @@ def tile_picked_lbm8_none_po_kernel(
             nc.vector.tensor_copy(xg[h][:], xw[:].bitcast(U32).indirect(offs_t[:, 16 * h : 16 * h + 16]))
 
         w1q.append(quant(w1g[1][:].rearrange("p t m j -> p (t m j)"), 256, "w1q1"))
-        w2g = placed([P, 4, P, 4], BF16, "w2g", 0)
+        w2g = on_vector([P, 4, P, 4], BF16, "w2g")
 
         def deal_w2(engine_copy, h, walk):
             a, n = w2_cuts[h]
@@ -136,75 +136,33 @@ def tile_picked_lbm8_none_po_kernel(
                 nc.scalar.copy(y[t][:], acc[:])
 
         deal_w2(gpsimd_copy, 1, "p t m j")
-        deal_w2(nc.scalar.copy, 2, "p m j t")
-        keep_rate = on_scalar([P, NP + NT], F32, "keep_rate")
-        nc.scalar.activation(keep_rate[:], rate[:], COPY, scale=-1.0, bias=1.0)
+        deal_w2(gpsimd_copy, 2, "p t m j")
+        keep_rate = on_gpsimd([P, NP + TURNED], F32, "keep_rate")
+        nc.gpsimd.tensor_scalar(keep_rate[:], rate[:], -1.0, 1.0, MULT, ADD)
 
         o_scales = keep.tile([P, S], U8, name="o_scales", align_bytes=64)
         out0_v = out_0.rearrange("(p t) j -> p t j", t=4)
         out1_v = out_1[0].rearrange("p n t -> p (n t)").bitcast(I32)
 
-        z, zb, zq, z_t, u_t, eq, o_t, back, outs, kept, moved, ob, o_codes, w2q = ({} for i in range(14))
+        z, zb, zq, z_t, u_t, eq, o_t, back, outs, kept, moved, ob, w2q = ({} for i in range(13))
 
-        def gather(first, count):
-            if first == 0:
-                dst = placed([P, 4, P * count], F32, "z0", 16)
-            else:
-                dst = on_vector([P, 4, P * count], F32, f"z{first}")
-            for t in range(4):
-                nc.vector.tensor_copy(dst[:, t, :], y[t][:].indirect(stream_t[:, 8 * first : 8 * (first + count)]))
-            if first == 0:
-                z["pair"] = dst[:]
-            for q in range(count):
-                z[first + q] = dst[:, :, P * q : P * q + P]
+        def planes(bank):
+            return bank[:].rearrange("p (t j) -> p t j", t=4)
 
-        def gather_two():
-            dst = [placed([P, 4, P], F32, "z0", 16), on_vector([P, 4, P], F32, "z1")]
-            for t in range(4):
-                for q in range(2):
-                    nc.vector.tensor_copy(dst[q][:, t, :], y[t][:].indirect(stream_t[:, 8 * q : 8 * q + 8]))
-            z[0], z[1] = dst[0][:], dst[1][:]
+        def along_cells(row, q):
+            first = (q - TURNED) * P
+            return row[:, first : first + P].unsqueeze(1).to_broadcast([P, 4, P])
 
-        def quant_w2():
-            w2q[0], w2q[1] = quant(w2g[:].rearrange("p t m j -> p (t m j)"), H, "w2q")
+        def gather(engine_copy, dst, t, first, count):
+            engine_copy(dst[:, t, :], y[t][:].indirect(stream_t[:, 8 * first : 8 * (first + count)]))
 
-        def round_z(q, engine_copy=nc.scalar.copy):
-            if q == 3:
-                zb[q] = placed([P, P, 4], BF16, "zb3", 8)
-            else:
-                zb[q] = on_scalar([P, P, 4], BF16, f"zb{q}")
-            interleave(engine_copy, zb[q][:], z[q])
+        def round_z(engine_copy, q):
+            interleave(engine_copy, zb[q], z[q])
 
-        def quant_z(q):
-            codes, scales = quant(zb[q][:].rearrange("p n t -> p (n t)"), P, f"zq{q}")
-            zq[q] = (codes[:], scales[:])
-
-        def round_z_pair():
-            zb[0] = on_scalar([P, 2 * P, 4], BF16, "zb01")
-            interleave(nc.scalar.copy, zb[0][:], z["pair"])
-
-        def quant_z_pair():
-            codes, scales = quant(zb[0][:].rearrange("p n t -> p (n t)"), 2 * P, "zq01")
-            for q in range(2):
-                zq[q] = (codes[:, P * q : P * q + P], scales[:, P * q : P * q + P])
-
-        def round_out_pair(q):
-            if "pair" not in ob:
-                ob["pair"] = on_scalar([P, 2 * P, 4], BF16, "ob01")
-            interleave(nc.scalar.copy, ob["pair"][:, P * q : P * q + P, :], outs[q][:])
-
-        def quant_out_pair():
-            o_codes[0] = on_vector([P, 256], I32, "o_codes0")
-            nc.vector.quantize_mx(
-                out=o_codes[0][:].bitcast(FP8X4),
-                scales=o_scales[:, 0 : 2 * P],
-                in_=ob["pair"][:].rearrange("p n t -> p (n t)"),
-            )
-            nc.sync.dma_start(out1_v[:, 0:256], o_codes[0][:])
-
-        def kept_free(q):
-            kept[q] = on_gpsimd([P, 4, P], F32, f"kept{q}")
-            nc.gpsimd.tensor_tensor(kept[q][:], z[q], along_cells(keep_rate, q), MULT)
+        def quant_z(first, count, tile):
+            codes, scales = quant(tile[:].rearrange("p n t -> p (n t)"), P * count, f"zq{first}")
+            for e in range(count):
+                zq[first + e] = (codes[:, P * e : P * e + P], scales[:, P * e : P * e + P])
 
         def turn_z(q):
             z_t[q] = psum.tile([P, 512], F32, name="acc")
@@ -244,128 +202,102 @@ def tile_picked_lbm8_none_po_kernel(
             o_t[q] = on_vector([P, 512], F32, f"o_t{q}")
             nc.vector.scalar_tensor_tensor(o_t[q][:], eq[q][:], rate[:, NP + q : NP + q + 1], u_t[q][:], MULT, ADD)
 
-        def moved_turned(q):
-            o_t[q] = on_scalar([P, 512], F32, f"e_t{q}")
-            nc.scalar.activation(o_t[q][:], eq[q][:], COPY, scale=rate[:, NP + q : NP + q + 1])
-
-        def turn_parts(q, parts, start, stop):
-            if start:
-                back[q] = psum.tile([P, 512], F32, name="acc")
-            for t in range(4):
-                for n, part in enumerate(parts):
-                    nc.tensor.matmul(
-                        back[q][:, P * t : P * t + P],
-                        part[:, P * t : P * t + P],
-                        ident[:],
-                        start=start and n == 0 and (t == 0 or stop),
-                        stop=stop and n == len(parts) - 1 and (t == 3 or start),
-                        is_transpose=True,
-                    )
-
-        def turn_back_sum(q):
-            turn_parts(q, (u_t[q], o_t[q]), True, True)
-
-        def turn_kept(q):
-            turn_parts(q, (u_t[q],), True, False)
-
-        def turn_moved(q):
-            turn_parts(q, (o_t[q],), False, True)
-
         def turn_back(q):
-            turn_parts(q, (o_t[q],), True, True)
+            back[q] = psum.tile([P, 512], F32, name="acc")
+            for t in range(4):
+                nc.tensor.transpose(back[q][:, P * t : P * t + P], o_t[q][:, P * t : P * t + P], ident[:])
 
         def store(q):
             nc.sync.dma_start(out0_v[:, :, q * P : q * P + P], outs[q][:])
 
         def leave_psum(q):
             outs[q] = on_scalar([P, 4, P], F32, f"o{q}")
-            nc.scalar.copy(outs[q][:], back[q][:].rearrange("p (t j) -> p t j", t=4))
+            nc.scalar.copy(outs[q][:], planes(back[q]))
             store(q)
 
-        def along_cells(row, q):
-            first = (q - NT) * P
-            return row[:, first : first + P].unsqueeze(1).to_broadcast([P, 4, P])
-
-        def kept_planes(q, kib):
-            kept[q] = placed([P, 4, P], F32, f"kept{q}", kib)
-            nc.gpsimd.tensor_tensor(kept[q][:], z[q], along_cells(keep_rate, q), MULT)
-
-        def kept_planes_vector(q):
+        def kept_planes(q):
             kept[q] = on_vector([P, 4, P], F32, f"kept{q}")
             nc.vector.tensor_tensor(kept[q][:], z[q], along_cells(keep_rate, q), MULT)
 
-        def relax_back(q):
-            outs[q] = on_vector([P, 4, P], F32, f"o{q}")
-            nc.vector.tensor_tensor(outs[q][:], back[q][:].rearrange("p (t j) -> p t j", t=4), kept[q][:], ADD)
-            store(q)
-
         def moved_planes(q):
             moved[q] = on_vector([P, 4, P], F32, f"moved{q}")
-            nc.vector.tensor_tensor(
-                moved[q][:], eq[q][:].rearrange("p (t j) -> p t j", t=4), along_cells(rate, q), MULT
-            )
+            nc.vector.tensor_tensor(moved[q][:], planes(eq[q]), along_cells(rate, q), MULT)
 
         def relax_planes(q):
             outs[q] = on_vector([P, 4, P], F32, f"o{q}")
             nc.vector.tensor_tensor(outs[q][:], moved[q][:], kept[q][:], ADD)
             store(q)
 
-        def round_out(q, engine_copy=nc.scalar.copy, make=on_scalar):
-            ob[q] = make([P, P, 4], BF16, f"ob{q}")
-            interleave(engine_copy, ob[q][:], outs[q][:])
-
-        def round_out_shared(q):
-            ob[q] = on_vector([P, P, 4], BF16, f"ob{q}")
-            interleave(nc.vector.tensor_copy, ob[q][:, 64:P, :], outs[q][:, :, 64:P])
-            interleave(nc.scalar.copy, ob[q][:, 0:64, :], outs[q][:, :, 0:64])
-
-        def quant_out(q, first, last):
+        def round_out(engine_copy, q):
             h, e = divmod(q, 2)
-            if first:
-                o_codes[h] = on_vector([P, 256], I32, f"o_codes{h}")
-            nc.vector.quantize_mx(
-                out=o_codes[h][:, P * e : P * e + P].bitcast(FP8X4),
-                scales=o_scales[:, P * q : P * q + P],
-                in_=ob[q][:].rearrange("p n t -> p (n t)"),
-            )
-            if last:
-                nc.sync.dma_start(out1_v[:, 256 * h : 256 * h + 256], o_codes[h][:])
+            if e == 0:
+                ob[h] = on_scalar([P, 2 * P, 4], BF16, f"ob{h}")
+            interleave(engine_copy, ob[h][:, P * e : P * e + P, :], outs[q][:])
 
-        gather(0, 2)
-        quant_w2()
+        def quant_out(h):
+            codes = on_vector([P, 2 * P], I32, f"o_codes{h}")
+            nc.vector.quantize_mx(
+                out=codes[:].bitcast(FP8X4),
+                scales=o_scales[:, 2 * P * h : 2 * P * h + 2 * P],
+                in_=ob[h][:].rearrange("p n t -> p (n t)"),
+            )
+            nc.sync.dma_start(out1_v[:, 2 * P * h : 2 * P * h + 2 * P], codes[:])
+
+        vector_copy = nc.vector.tensor_copy
+        z01 = on_vector([P, 4, 2 * P], F32, "z01")
+        for t in range(4):
+            gather(vector_copy, z01, t, 0, 2)
+        z[0], z[1] = z01[:, :, 0:P], z01[:, :, P : 2 * P]
+        z2 = on_scalar([P, 4, P], F32, "z2")
+        for t in range(4):
+            gather(scalar_copy, z2, t, 2, 1)
+        z[2] = z2[:]
+        z3 = on_vector([P, 4, P], F32, "z3")
+        z[3] = z3[:]
+        gather(vector_copy, z3, 0, 3, 1)
+        zb01 = on_vector([P, 2 * P, 4], BF16, "zb01")
+        zb[0], zb[1] = zb01[:, 0:P, :], zb01[:, P : 2 * P, :]
+        round_z(vector_copy, 1)
+        round_z(nc.scalar.copy, 0)
+        w2q[0], w2q[1] = quant(w2g[:].rearrange("p t m j -> p (t m j)"), H, "w2q")
         turn_z(0)
-        round_z_pair()
-        gather(2, 1)
-        kept_free(1)
-        quant_z_pair()
+        turn_z(1)
+        gather(scalar_copy, z3, 1, 3, 1)
+        gather(scalar_copy, z3, 2, 3, 1)
+        quant_z(0, 2, zb01)
         kept_turned(0)
-        round_z(2)
+        gather(scalar_copy, z3, 3, 3, 1)
+        zb2 = on_vector([P, P, 4], BF16, "zb2")
+        zb[2] = zb2[:]
+        round_z(vector_copy, 2)
         product_turned(0)
-        product_planes(1)
-        gather(3, 1)
-        kept_free(2)
-        quant_z(2)
-        round_z(3)
-        relax_turned(0)
+        product_turned(1)
+        kept_planes(2)
+        kept_turned(1)
+        quant_z(2, 1, zb2)
+        zb3 = on_scalar([P, P, 4], BF16, "zb3")
+        zb[3] = zb3[:]
+        round_z(nc.scalar.copy, 3)
         product_planes(2)
-        moved_planes(1)
+        relax_turned(0)
+        relax_turned(1)
         turn_back(0)
-        quant_z(3)
-        kept_planes(3, 8)
+        turn_back(1)
+        quant_z(3, 1, zb3)
+        kept_planes(3)
         product_planes(3)
-        relax_planes(1)
-        moved_planes(2)
         leave_psum(0)
+        leave_psum(1)
+        moved_planes(2)
         moved_planes(3)
-        round_out_pair(1)
-        round_out_pair(0)
+        round_out(nc.scalar.copy, 0)
+        round_out(nc.scalar.copy, 1)
         relax_planes(2)
         relax_planes(3)
-        round_out(2)
-        quant_out_pair()
-        round_out_shared(3)
-        quant_out(2, True, False)
-        quant_out(3, False, True)
+        round_out(nc.scalar.copy, 2)
+        quant_out(0)
+        round_out(vector_copy, 3)
+        quant_out(1)
         for q in range(4):
             (nc.scalar, nc.sync)[q % 2].dma_start(
                 out_2[0, q:16:4, :].bitcast(I32), o_scales[q:P:32, :].bitcast(I32)

@@ -87,7 +87,7 @@ def tile_picked_lbm8_none_po_kernel(
         nc.vector.tensor_copy(xg_s[:], xs[:].indirect(offs_t[:]))
 
         w2_rows = w2.rearrange("(p j) c -> p j c", j=4)
-        w2_cuts = ((0, 128), (128, 256), (384, 128))
+        w2_cuts = ((0, 256), (256, 128), (384, 128))
         w2_raw = [keep.tile([P, 4, n], F32, name=f"w2_raw{h}") for h, (a, n) in enumerate(w2_cuts)]
         for h in range(3):
             a, n = w2_cuts[h]
@@ -137,14 +137,12 @@ def tile_picked_lbm8_none_po_kernel(
 
         deal_w2(gpsimd_copy, 1, "p t m j")
         deal_w2(gpsimd_copy, 2, "p t m j")
-        keep_rate = on_gpsimd([P, NP + TURNED], F32, "keep_rate")
-        nc.gpsimd.tensor_scalar(keep_rate[:], rate[:], -1.0, 1.0, MULT, ADD)
 
         o_scales = keep.tile([P, S], U8, name="o_scales", align_bytes=64)
         out0_v = out_0.rearrange("(p t) j -> p t j", t=4)
         out1_v = out_1[0].rearrange("p n t -> p (n t)").bitcast(I32)
 
-        z, zb, zq, z_t, u_t, eq, o_t, back, outs, kept, moved, ob, w2q = ({} for i in range(13))
+        z, zb, zq, z_t, u_t, eq, o_t, back, outs, kept, moved, ob, w2q, o_codes = ({} for i in range(14))
 
         def planes(bank):
             return bank[:].rearrange("p (t j) -> p t j", t=4)
@@ -234,14 +232,17 @@ def tile_picked_lbm8_none_po_kernel(
                 ob[h] = on_scalar([P, 2 * P, 4], BF16, f"ob{h}")
             interleave(engine_copy, ob[h][:, P * e : P * e + P, :], outs[q][:])
 
-        def quant_out(h):
-            codes = on_vector([P, 2 * P], I32, f"o_codes{h}")
+        def quant_out(first, count):
+            h, e = divmod(first, 2)
+            if e == 0:
+                o_codes[h] = on_vector([P, 2 * P], I32, f"o_codes{h}")
             nc.vector.quantize_mx(
-                out=codes[:].bitcast(FP8X4),
-                scales=o_scales[:, 2 * P * h : 2 * P * h + 2 * P],
-                in_=ob[h][:].rearrange("p n t -> p (n t)"),
+                out=o_codes[h][:, P * e : P * (e + count)].bitcast(FP8X4),
+                scales=o_scales[:, P * first : P * (first + count)],
+                in_=ob[h][:, P * e : P * (e + count), :].rearrange("p n t -> p (n t)"),
             )
-            nc.sync.dma_start(out1_v[:, 2 * P * h : 2 * P * h + 2 * P], codes[:])
+            if e + count == 2:
+                nc.sync.dma_start(out1_v[:, 2 * P * h : 2 * P * h + 2 * P], o_codes[h][:])
 
         vector_copy = nc.vector.tensor_copy
         z01 = on_vector([P, 4, 2 * P], F32, "z01")
@@ -252,7 +253,7 @@ def tile_picked_lbm8_none_po_kernel(
         for t in range(4):
             gather(scalar_copy, z2, t, 2, 1)
         z[2] = z2[:]
-        z3 = on_vector([P, 4, P], F32, "z3")
+        z3 = on_scalar([P, 4, P], F32, "z3")
         z[3] = z3[:]
         gather(vector_copy, z3, 0, 3, 1)
         zb01 = on_vector([P, 2 * P, 4], BF16, "zb01")
@@ -260,6 +261,8 @@ def tile_picked_lbm8_none_po_kernel(
         round_z(vector_copy, 1)
         round_z(nc.scalar.copy, 0)
         w2q[0], w2q[1] = quant(w2g[:].rearrange("p t m j -> p (t m j)"), H, "w2q")
+        keep_rate = on_vector([P, NP + TURNED], F32, "keep_rate")
+        nc.vector.tensor_scalar(keep_rate[:], rate[:], -1.0, 1.0, MULT, ADD)
         turn_z(0)
         turn_z(1)
         gather(scalar_copy, z3, 1, 3, 1)
@@ -295,9 +298,10 @@ def tile_picked_lbm8_none_po_kernel(
         relax_planes(2)
         relax_planes(3)
         round_out(nc.scalar.copy, 2)
-        quant_out(0)
+        quant_out(0, 2)
         round_out(vector_copy, 3)
-        quant_out(1)
+        quant_out(2, 1)
+        quant_out(3, 1)
         for q in range(4):
             (nc.scalar, nc.sync)[q % 2].dma_start(
                 out_2[0, q:16:4, :].bitcast(I32), o_scales[q:P:32, :].bitcast(I32)

@@ -246,23 +246,25 @@ def tile_picked_lbm8_none_po_kernel(
 
         vector_copy = nc.vector.tensor_copy
         z01 = on_vector([P, 4, 2 * P], F32, "z01")
-        for t in range(4):
+        for t in range(3):
             gather(vector_copy, z01, t, 0, 2)
+        for q in range(2):
+            gather(vector_copy, z01[:, :, P * q : P * q + P], 3, q, 1)
         z[0], z[1] = z01[:, :, 0:P], z01[:, :, P : 2 * P]
         z2 = on_scalar([P, 4, P], F32, "z2")
         for t in range(4):
             gather(scalar_copy, z2, t, 2, 1)
         z[2] = z2[:]
-        z3 = on_scalar([P, 4, P], F32, "z3")
-        z[3] = z3[:]
-        gather(vector_copy, z3, 0, 3, 1)
         zb01 = on_vector([P, 2 * P, 4], BF16, "zb01")
         zb[0], zb[1] = zb01[:, 0:P, :], zb01[:, P : 2 * P, :]
-        round_z(vector_copy, 1)
-        round_z(nc.scalar.copy, 0)
+        round_z(vector_copy, 0)
+        round_z(nc.scalar.copy, 1)
         w2q[0], w2q[1] = quant(w2g[:].rearrange("p t m j -> p (t m j)"), H, "w2q")
         keep_rate = on_vector([P, NP + TURNED], F32, "keep_rate")
         nc.vector.tensor_scalar(keep_rate[:], rate[:], -1.0, 1.0, MULT, ADD)
+        z3 = on_vector([P, 4, P], F32, "z3")
+        z[3] = z3[:]
+        gather(vector_copy, z3, 0, 3, 1)
         turn_z(0)
         turn_z(1)
         gather(scalar_copy, z3, 1, 3, 1)

@@ -142,7 +142,7 @@ def tile_picked_lbm8_none_po_kernel(
         out0_v = out_0.rearrange("(p t) j -> p t j", t=4)
         out1_v = out_1[0].rearrange("p n t -> p (n t)").bitcast(I32)
 
-        z, zb, zq, z_t, u_t, eq, o_t, back, outs, kept, moved, ob, w2q, o_codes = ({} for i in range(14))
+        z, zb, zq, z_t, u_t, eq, o_t, back, outs, kept, moved, ob, w2q, o_codes, work = ({} for i in range(15))
 
         def planes(bank):
             return bank[:].rearrange("p (t j) -> p t j", t=4)
@@ -154,13 +154,14 @@ def tile_picked_lbm8_none_po_kernel(
         def gather(engine_copy, dst, t, first, count):
             engine_copy(dst[:, t, :], y[t][:].indirect(stream_t[:, 8 * first : 8 * (first + count)]))
 
-        def round_z(engine_copy, q):
-            interleave(engine_copy, zb[q], z[q])
+        def round_z(engine_copy, make, q):
+            work[q] = make([P, 4 * P], F32, f"work{q}")
+            zb[q] = work[q][:].bitcast(BF16)[:, 0 : 4 * P]
+            interleave(engine_copy, zb[q].rearrange("p (n t) -> p n t", t=4), z[q])
 
-        def quant_z(first, count, tile):
-            codes, scales = quant(tile[:].rearrange("p n t -> p (n t)"), P * count, f"zq{first}")
-            for e in range(count):
-                zq[first + e] = (codes[:, P * e : P * e + P], scales[:, P * e : P * e + P])
+        def quant_z(q):
+            codes, scales = quant(zb[q], P, f"zq{q}")
+            zq[q] = (codes[:], scales[:])
 
         def turn_z(q):
             z_t[q] = psum.tile([P, 512], F32, name="acc")
@@ -214,8 +215,8 @@ def tile_picked_lbm8_none_po_kernel(
             store(q)
 
         def kept_planes(q):
-            kept[q] = on_vector([P, 4, P], F32, f"kept{q}")
-            nc.vector.tensor_tensor(kept[q][:], z[q], along_cells(keep_rate, q), MULT)
+            kept[q] = planes(work[q])
+            nc.gpsimd.tensor_tensor(kept[q], z[q], along_cells(keep_rate, q), MULT)
 
         def moved_planes(q):
             moved[q] = on_vector([P, 4, P], F32, f"moved{q}")
@@ -223,7 +224,7 @@ def tile_picked_lbm8_none_po_kernel(
 
         def relax_planes(q):
             outs[q] = on_vector([P, 4, P], F32, f"o{q}")
-            nc.vector.tensor_tensor(outs[q][:], moved[q][:], kept[q][:], ADD)
+            nc.vector.tensor_tensor(outs[q][:], moved[q][:], kept[q], ADD)
             store(q)
 
         def round_out(engine_copy, q):
@@ -252,43 +253,39 @@ def tile_picked_lbm8_none_po_kernel(
             gather(vector_copy, z01[:, :, P * q : P * q + P], 3, q, 1)
         z[0], z[1] = z01[:, :, 0:P], z01[:, :, P : 2 * P]
         z2 = on_scalar([P, 4, P], F32, "z2")
-        for t in range(4):
+        for t in range(3):
             gather(scalar_copy, z2, t, 2, 1)
+        gather(vector_copy, z2, 3, 2, 1)
         z[2] = z2[:]
-        zb01 = on_vector([P, 2 * P, 4], BF16, "zb01")
-        zb[0], zb[1] = zb01[:, 0:P, :], zb01[:, P : 2 * P, :]
-        round_z(vector_copy, 0)
-        round_z(nc.scalar.copy, 1)
+        keep_rate = on_scalar([P, NP + TURNED], F32, "keep_rate")
+        nc.scalar.activation(keep_rate[:], rate[:], COPY, scale=-1.0, bias=1.0)
+        round_z(vector_copy, on_vector, 0)
+        round_z(nc.scalar.copy, on_scalar, 1)
         w2q[0], w2q[1] = quant(w2g[:].rearrange("p t m j -> p (t m j)"), H, "w2q")
-        keep_rate = on_vector([P, NP + TURNED], F32, "keep_rate")
-        nc.vector.tensor_scalar(keep_rate[:], rate[:], -1.0, 1.0, MULT, ADD)
-        z3 = on_vector([P, 4, P], F32, "z3")
-        z[3] = z3[:]
-        gather(vector_copy, z3, 0, 3, 1)
         turn_z(0)
         turn_z(1)
+        z3 = on_scalar([P, 4, P], F32, "z3")
+        z[3] = z3[:]
         gather(scalar_copy, z3, 1, 3, 1)
         gather(scalar_copy, z3, 2, 3, 1)
-        quant_z(0, 2, zb01)
+        quant_z(0)
+        round_z(vector_copy, on_vector, 2)
+        quant_z(1)
         kept_turned(0)
         gather(scalar_copy, z3, 3, 3, 1)
-        zb2 = on_vector([P, P, 4], BF16, "zb2")
-        zb[2] = zb2[:]
-        round_z(vector_copy, 2)
+        gather(vector_copy, z3, 0, 3, 1)
         product_turned(0)
         product_turned(1)
-        kept_planes(2)
         kept_turned(1)
-        quant_z(2, 1, zb2)
-        zb3 = on_scalar([P, P, 4], BF16, "zb3")
-        zb[3] = zb3[:]
-        round_z(nc.scalar.copy, 3)
+        quant_z(2)
+        kept_planes(2)
+        round_z(nc.scalar.copy, on_scalar, 3)
         product_planes(2)
         relax_turned(0)
         relax_turned(1)
         turn_back(0)
         turn_back(1)
-        quant_z(3, 1, zb3)
+        quant_z(3)
         kept_planes(3)
         product_planes(3)
         leave_psum(0)

@@ -116,9 +116,17 @@ def tile_picked_lbm8_none_po_kernel(
 
         deal_w2(nc.vector.tensor_copy, 0, "p m j t")
 
-        y = [on_scalar([P, S], F32, f"y{t}") for t in range(4)]
+        def gather(engine_copy, dst, t, first, count):
+            engine_copy(dst[:, t, :], y[t][:].indirect(stream_t[:, 8 * first : 8 * (first + count)]))
+
+        y = {}
         for t, h in ((0, 0), (1, 0), (0, 1), (1, 1), (2, 0), (2, 1), (3, 0), (3, 1)):
             u, e = divmod(t, 2)
+            if (t, h) == (2, 0):
+                z2 = on_scalar([P, 4, P], F32, "z2")
+                gather(scalar_copy, z2, 0, 2, 1)
+            if h == 0:
+                y[t] = on_scalar([P, S], F32, f"y{t}")
             if t < 2 or h == 0:
                 acc = psum.tile([P, 512], F32, name="acc")
             nc.tensor.matmul_mx(
@@ -150,9 +158,6 @@ def tile_picked_lbm8_none_po_kernel(
         def along_cells(row, q):
             first = (q - TURNED) * P
             return row[:, first : first + P].unsqueeze(1).to_broadcast([P, 4, P])
-
-        def gather(engine_copy, dst, t, first, count):
-            engine_copy(dst[:, t, :], y[t][:].indirect(stream_t[:, 8 * first : 8 * (first + count)]))
 
         def round_z(engine_copy, make, q):
             work[q] = make([P, 4 * P], F32, f"work{q}")
@@ -231,7 +236,10 @@ def tile_picked_lbm8_none_po_kernel(
             h, e = divmod(q, 2)
             if e == 0:
                 ob[h] = on_scalar([P, 2 * P, 4], BF16, f"ob{h}")
-            interleave(engine_copy, ob[h][:, P * e : P * e + P, :], outs[q][:])
+            if q < TURNED:
+                engine_copy(ob[h][:, P * e : P * e + P, :], planes(back[q]).rearrange("p t c -> p c t"))
+            else:
+                interleave(engine_copy, ob[h][:, P * e : P * e + P, :], outs[q][:])
 
         def quant_out(first, count):
             h, e = divmod(first, 2)
@@ -252,8 +260,7 @@ def tile_picked_lbm8_none_po_kernel(
         for q in range(2):
             gather(vector_copy, z01[:, :, P * q : P * q + P], 3, q, 1)
         z[0], z[1] = z01[:, :, 0:P], z01[:, :, P : 2 * P]
-        z2 = on_scalar([P, 4, P], F32, "z2")
-        for t in range(3):
+        for t in (1, 2):
             gather(scalar_copy, z2, t, 2, 1)
         gather(vector_copy, z2, 3, 2, 1)
         z[2] = z2[:]
@@ -264,20 +271,19 @@ def tile_picked_lbm8_none_po_kernel(
         w2q[0], w2q[1] = quant(w2g[:].rearrange("p t m j -> p (t m j)"), H, "w2q")
         turn_z(0)
         turn_z(1)
-        z3 = on_scalar([P, 4, P], F32, "z3")
-        z[3] = z3[:]
-        gather(scalar_copy, z3, 1, 3, 1)
-        gather(scalar_copy, z3, 2, 3, 1)
+        z[3] = planes(work[1])
+        gather(scalar_copy, z[3], 2, 3, 1)
+        gather(scalar_copy, z[3], 3, 3, 1)
         quant_z(0)
         round_z(vector_copy, on_vector, 2)
         quant_z(1)
         kept_turned(0)
-        gather(scalar_copy, z3, 3, 3, 1)
-        gather(vector_copy, z3, 0, 3, 1)
         product_turned(0)
         product_turned(1)
         kept_turned(1)
         quant_z(2)
+        gather(vector_copy, z[3], 0, 3, 1)
+        gather(vector_copy, z[3], 1, 3, 1)
         kept_planes(2)
         round_z(nc.scalar.copy, on_scalar, 3)
         product_planes(2)
@@ -286,11 +292,13 @@ def tile_picked_lbm8_none_po_kernel(
         turn_back(0)
         turn_back(1)
         quant_z(3)
-        kept_planes(3)
         product_planes(3)
         leave_psum(0)
         leave_psum(1)
         moved_planes(2)
+        kept3 = on_vector([P, 4, P], F32, "kept3")
+        kept[3] = kept3[:]
+        nc.vector.tensor_tensor(kept[3], z[3], along_cells(keep_rate, 3), MULT)
         moved_planes(3)
         round_out(nc.scalar.copy, 0)
         round_out(nc.scalar.copy, 1)

@@ -260,15 +260,14 @@ def tile_picked_lbm8_none_po_kernel(
         for q in range(2):
             gather(vector_copy, z01[:, :, P * q : P * q + P], 3, q, 1)
         z[0], z[1] = z01[:, :, 0:P], z01[:, :, P : 2 * P]
-        for t in (1, 2):
+        for t in (1, 2, 3):
             gather(scalar_copy, z2, t, 2, 1)
-        gather(vector_copy, z2, 3, 2, 1)
         z[2] = z2[:]
-        keep_rate = on_scalar([P, NP + TURNED], F32, "keep_rate")
-        nc.scalar.activation(keep_rate[:], rate[:], COPY, scale=-1.0, bias=1.0)
         round_z(vector_copy, on_vector, 0)
         round_z(nc.scalar.copy, on_scalar, 1)
         w2q[0], w2q[1] = quant(w2g[:].rearrange("p t m j -> p (t m j)"), H, "w2q")
+        keep_rate = on_vector([P, NP + TURNED], F32, "keep_rate")
+        nc.vector.tensor_scalar(keep_rate[:], rate[:], -1.0, 1.0, MULT, ADD)
         turn_z(0)
         turn_z(1)
         z[3] = planes(work[1])

@@ -17,6 +17,7 @@ COPY = mybir.ActivationFunctionType.Copy
 P = 128
 K, T, S, H = 512, 2048, 512, 512
 FLOPS = 2 * 2 * 512 * 512 * 512
+HALF = 256
 TURNED = 2
 
 
@@ -27,36 +28,18 @@ def tile_picked_lbm8_none_po_kernel(
     with ExitStack() as ctx:
         keep = ctx.enter_context(tc.tile_pool(name="keep", bufs=1))
         queue = ctx.enter_context(tc.tile_pool(name="queue", bufs=1))
-        shared = ctx.enter_context(tc.tile_pool(name="shared", bufs=1))
         psum = ctx.enter_context(tc.psum_pool(name="psum", bufs=8))
 
         def on_vector(shape, dtype, name):
-            return queue.tile(shape, dtype, name=name, tag="vector", bufs=26, align_bytes=64)
+            return queue.tile(shape, dtype, name=name, tag="vector", bufs=30, align_bytes=64)
 
         def on_scalar(shape, dtype, name):
             return queue.tile(shape, dtype, name=name, tag="scalar", bufs=20, align_bytes=64)
 
-        def on_gpsimd(shape, dtype, name):
-            return queue.tile(shape, dtype, name=name, tag="gpsimd", bufs=4, align_bytes=64)
+        def bank():
+            return psum.tile([P, 512], F32, name="bank")
 
-        def placed(shape, dtype, name, kib):
-            return shared.tile(shape, dtype, name=name, offset=1024 * kib, align_bytes=64)
-
-        offs_t = keep.tile([P, S // 16], U16, name="offs_t")
-        stream_t = keep.tile([P, S // 16], U16, name="stream_t")
-        xw = keep.tile([P, T], I32, name="xw")
-        xs = keep.tile([P, T], U8, name="xs")
-        w1_raw = keep.tile([P, 4, H], F32, name="w1_raw")
-        ident = keep.tile([P, P], F32, name="ident")
-
-        nc.vector.memset(xs[:].bitcast(I32), 0)
-        nc.sync.dma_start(w1_raw[:], w1.rearrange("(p j) c -> p j c", j=4))
-        nc.sync.dma_start(offs_t[:], offs)
-        for q in range(4):
-            nc.sync.dma_start(xs[q:P:32, :].bitcast(I32), x_scales[0, q:16:4, :].bitcast(I32))
-        nc.sync.dma_start(xw[:], x_words[0].rearrange("p n t -> p (n t)").bitcast(I32))
-        nc.sync.dma_start(stream_t[:], stream)
-        make_identity(nc, ident[:])
+        vector_copy = nc.vector.tensor_copy
 
         def scalar_copy(dst, src):
             nc.scalar.activation(dst, src, COPY)
@@ -64,150 +47,156 @@ def tile_picked_lbm8_none_po_kernel(
         def gpsimd_copy(dst, src):
             nc.gpsimd.tensor_scalar(dst, src, 1.0, 0.0, MULT, ADD)
 
-        def deal(engine_copy, make, u):
-            grouped = make([P, 2, P, 4], BF16, f"w1g{u}")
-            engine_copy(
-                grouped[:].rearrange("p t m j -> p m j t"),
-                w1_raw[:].rearrange("p j (m t) -> p m j t", t=4)[:, :, :, 2 * u : 2 * u + 2],
-            )
-            return grouped
+        def quantise(codes, scales, values):
+            nc.vector.quantize_mx(out=codes.bitcast(FP8X4), scales=scales, in_=values)
 
-        def quant(grouped_flat, width, name):
-            codes = on_vector([P, width], U32, name + "_c")
-            scales = keep.tile([P, width], U8, name=name + "_s", align_bytes=64)
-            nc.vector.quantize_mx(out=codes[:].bitcast(FP8X4), scales=scales[:], in_=grouped_flat)
-            return codes, scales
-
-        def interleave(engine_copy, dst, src):
-            engine_copy(dst.rearrange("p (c i) t -> p c t i", i=4), src.rearrange("p t (c i) -> p c t i", i=4))
-
-        w1g = [deal(nc.vector.tensor_copy, on_vector, 0), deal(scalar_copy, on_scalar, 1)]
-        w1q = [quant(w1g[0][:].rearrange("p t m j -> p (t m j)"), 256, "w1q0")]
-        xg_s = on_vector([P, S], U8, "xg_s")
-        nc.vector.tensor_copy(xg_s[:], xs[:].indirect(offs_t[:]))
-
-        w2_rows = w2.rearrange("(p j) c -> p j c", j=4)
-        w2_cuts = ((0, 256), (256, 128), (384, 128))
-        w2_raw = [keep.tile([P, 4, n], F32, name=f"w2_raw{h}") for h, (a, n) in enumerate(w2_cuts)]
-        for h in range(3):
-            a, n = w2_cuts[h]
-            nc.sync.dma_start(w2_raw[h][:], w2_rows[:, :, a : a + n])
-
-        NP = S - P * TURNED
-        rate = keep.tile([P, NP + TURNED], F32, name="rate")
-        nc.sync.dma_start(rate[:, 0:NP], om[:, P * TURNED : S])
-        with nc.allow_non_contiguous_dma(reason="one rate for each partition"):
-            nc.sync.dma_start(rate[:, NP : NP + TURNED], om[0, 0 : P * TURNED].rearrange("(q p) -> p q", p=P))
-
-        xg = []
-        for h in range(2):
-            xg.append(on_vector([P, 256], U32, f"xg{h}"))
-            nc.vector.tensor_copy(xg[h][:], xw[:].bitcast(U32).indirect(offs_t[:, 16 * h : 16 * h + 16]))
-
-        w1q.append(quant(w1g[1][:].rearrange("p t m j -> p (t m j)"), 256, "w1q1"))
-        w2g = on_vector([P, 4, P, 4], BF16, "w2g")
-
-        def deal_w2(engine_copy, h, walk):
-            a, n = w2_cuts[h]
-            engine_copy(
-                w2g[:, :, a // 4 : (a + n) // 4, :].rearrange("p t m j -> " + walk),
-                w2_raw[h][:].rearrange("p j (m t) -> " + walk, t=4),
-            )
-
-        deal_w2(nc.vector.tensor_copy, 0, "p m j t")
-
-        def gather(engine_copy, dst, t, first, count):
-            engine_copy(dst[:, t, :], y[t][:].indirect(stream_t[:, 8 * first : 8 * (first + count)]))
-
-        y = {}
-        for t, h in ((0, 0), (1, 0), (0, 1), (1, 1), (2, 0), (2, 1), (3, 0), (3, 1)):
-            u, e = divmod(t, 2)
-            if (t, h) == (2, 0):
-                z2 = on_scalar([P, 4, P], F32, "z2")
-                gather(scalar_copy, z2, 0, 2, 1)
-            if h == 0:
-                y[t] = on_scalar([P, S], F32, f"y{t}")
-            if t < 2 or h == 0:
-                acc = psum.tile([P, 512], F32, name="acc")
+        def product(out, still, moving):
             nc.tensor.matmul_mx(
-                out=acc[:, 256 * h : 256 * h + 256],
-                lhsT=w1q[u][0][:, P * e : P * e + P].bitcast(FP8X4),
-                lhsT_scale=w1q[u][1][:, P * e : P * e + P],
-                rhs=xg[h][:].bitcast(FP8X4),
-                rhs_scale=xg_s[:, 256 * h : 256 * h + 256],
+                out=out,
+                lhsT=still[0].bitcast(FP8X4),
+                lhsT_scale=still[1],
+                rhs=moving[0].bitcast(FP8X4),
+                rhs_scale=moving[1],
                 start=True,
                 stop=True,
             )
-            if t < 2:
-                nc.scalar.copy(y[t][:, 256 * h : 256 * h + 256], acc[:, 256 * h : 256 * h + 256])
-            elif h == 1:
-                nc.scalar.copy(y[t][:], acc[:])
 
-        deal_w2(gpsimd_copy, 1, "p t m j")
-        deal_w2(gpsimd_copy, 2, "p t m j")
+        def columns(pair, first, count):
+            return pair[0][:, first : first + count], pair[1][:, first : first + count]
+
+        offs_t = keep.tile([P, S // 16], U16, name="offs_t")
+        stream_t = keep.tile([P, S // 16], U16, name="stream_t")
+        xw = keep.tile([P, T], I32, name="xw")
+        xs = keep.tile([P, T], U8, name="xs")
+        ident = keep.tile([P, P], F32, name="ident")
+
+        w1_raw = [keep.tile([P, 4, HALF], F32, name=f"w1_raw{h}") for h in range(2)]
+        nc.vector.memset(xs[:].bitcast(I32), 0)
+        w1_rows = w1.rearrange("(p j) c -> p j c", j=4)
+        nc.sync.dma_start(w1_raw[0][:], w1_rows[:, :, 0:HALF])
+        nc.sync.dma_start(offs_t[:], offs)
+        for r in range(4):
+            nc.sync.dma_start(xs[r:P:32, :].bitcast(I32), x_scales[0, r:16:4, :].bitcast(I32))
+        nc.sync.dma_start(w1_raw[1][:], w1_rows[:, :, HALF:H])
+        nc.sync.dma_start(xw[:], x_words[0].rearrange("p n t -> p (n t)").bitcast(I32))
+        nc.sync.dma_start(stream_t[:], stream)
+        w2_rows = w2.rearrange("(p j) c -> p j c", j=4)
+        w2_cuts = ((0, HALF), (HALF, P), (HALF + P, P))
+        w2_raw = [keep.tile([P, 4, n], F32, name=f"w2_raw{i}") for i, (a, n) in enumerate(w2_cuts)]
+        for i, (a, n) in enumerate(w2_cuts):
+            nc.sync.dma_start(w2_raw[i][:], w2_rows[:, :, a : a + n])
+        along = S - P * TURNED
+        rate = keep.tile([P, along + TURNED], F32, name="rate")
+        nc.sync.dma_start(rate[:, 0:along], om[:, P * TURNED : S])
+        with nc.allow_non_contiguous_dma(reason="one rate for each partition"):
+            nc.sync.dma_start(rate[:, along : along + TURNED], om[0, 0 : P * TURNED].rearrange("(q p) -> p q", p=P))
+        make_identity(nc, ident[:])
+
+        def round_w1(engine_copy, u, h):
+            engine_copy(
+                w1g[u][:, :, 64 * h : 64 * h + 64, :].rearrange("p t m j -> p m j t"),
+                w1_raw[h][:].rearrange("p j (m t) -> p m j t", t=4)[:, :, :, 2 * u : 2 * u + 2],
+            )
+
+        def quantise_w1(grouped, u):
+            pair = (on_vector([P, HALF], U32, f"w1_codes{u}"), keep.tile([P, HALF], U8, name=f"w1_scales{u}", align_bytes=64))
+            quantise(pair[0][:], pair[1][:], grouped[:].rearrange("p t m j -> p (t m j)"))
+            return pair
+
+        w1g = [on_vector([P, 2, P, 4], BF16, "w1g0"), on_scalar([P, 2, P, 4], BF16, "w1g1")]
+        round_w1(vector_copy, 0, 0)
+        round_w1(scalar_copy, 1, 0)
+        xg_scales = on_vector([P, S], U8, "xg_scales")
+        vector_copy(xg_scales[:], xs[:].indirect(offs_t[:]))
+        round_w1(vector_copy, 0, 1)
+        round_w1(scalar_copy, 1, 1)
+        w1q = [quantise_w1(w1g[u], u) for u in range(2)]
+        xq = []
+        for h in range(2):
+            words = on_vector([P, HALF], U32, f"xg_words{h}")
+            vector_copy(words[:], xw[:].bitcast(U32).indirect(offs_t[:, 16 * h : 16 * h + 16]))
+            xq.append((words[:], xg_scales[:, HALF * h : HALF * h + HALF]))
+
+        y = {}
+        for t, h in ((0, 0), (1, 0), (0, 1), (1, 1), (2, 0), (2, 1), (3, 0), (3, 1)):
+            if h == 0:
+                y[t] = on_scalar([P, S], F32, f"y{t}")
+            acc = bank()
+            product(acc[:, 0:HALF], columns(w1q[t // 2], P * (t % 2), P), xq[h])
+            nc.scalar.copy(y[t][:, HALF * h : HALF * h + HALF], acc[:, 0:HALF])
+
+        w2g = [on_vector([P, 4, HALF // 4, 4], BF16, f"w2g{h}") for h in range(2)]
+
+        def round_w2(engine_copy, i, walk):
+            a, n = w2_cuts[i]
+            h, first = divmod(a, HALF)
+            engine_copy(
+                w2g[h][:, :, first // 4 : (first + n) // 4, :].rearrange("p t m j -> " + walk),
+                w2_raw[i][:].rearrange("p j (m t) -> " + walk, t=4),
+            )
+
+        w2q = (keep.tile([P, H], U32, name="w2_codes", align_bytes=64), keep.tile([P, H], U8, name="w2_scales", align_bytes=64))
+
+        def quantise_w2(h):
+            for t in range(4):
+                quantise(*columns(w2q, P * t + 64 * h, 64), w2g[h][:, t, :, :].rearrange("p m j -> p (m j)"))
+
+        round_w2(vector_copy, 0, "p m j t")
+        round_w2(vector_copy, 1, "p m j t")
+        quantise_w2(0)
+        round_w2(gpsimd_copy, 2, "p t m j")
 
         o_scales = keep.tile([P, S], U8, name="o_scales", align_bytes=64)
         out0_v = out_0.rearrange("(p t) j -> p t j", t=4)
         out1_v = out_1[0].rearrange("p n t -> p (n t)").bitcast(I32)
+        z, zb, zq, z_t, u_t, eq, o_t, back, outs, kept, moved, ob, o_codes, work = ({} for i in range(14))
 
-        z, zb, zq, z_t, u_t, eq, o_t, back, outs, kept, moved, ob, w2q, o_codes, work = ({} for i in range(15))
-
-        def planes(bank):
-            return bank[:].rearrange("p (t j) -> p t j", t=4)
+        def planes(tile):
+            return tile[:].rearrange("p (t j) -> p t j", t=4)
 
         def along_cells(row, q):
             first = (q - TURNED) * P
             return row[:, first : first + P].unsqueeze(1).to_broadcast([P, 4, P])
+
+        def interleave(engine_copy, dst, src):
+            engine_copy(dst.rearrange("p (c i) t -> p c t i", i=4), src.rearrange("p t (c i) -> p c t i", i=4))
+
+        def gather(engine_copy, dst, t, first, count):
+            engine_copy(dst[:, t, :], y[t][:].indirect(stream_t[:, 8 * first : 8 * (first + count)]))
 
         def round_z(engine_copy, make, q):
             work[q] = make([P, 4 * P], F32, f"work{q}")
             zb[q] = work[q][:].bitcast(BF16)[:, 0 : 4 * P]
             interleave(engine_copy, zb[q].rearrange("p (n t) -> p n t", t=4), z[q])
 
-        def quant_z(q):
-            codes, scales = quant(zb[q], P, f"zq{q}")
-            zq[q] = (codes[:], scales[:])
+        def quantise_z(q):
+            zq[q] = (on_vector([P, P], U32, f"z_codes{q}")[:], keep.tile([P, P], U8, name=f"z_scales{q}", align_bytes=64)[:])
+            quantise(*zq[q], zb[q])
 
         def turn_z(q):
-            z_t[q] = psum.tile([P, 512], F32, name="acc")
+            z_t[q] = bank()
             for t in range(4):
                 nc.tensor.transpose(z_t[q][:, P * t : P * t + P], z[q][:, t, :], ident[:])
 
         def kept_turned(q):
             u_t[q] = on_scalar([P, 512], F32, f"u_t{q}")
-            nc.scalar.activation(u_t[q][:], z_t[q][:], COPY, scale=keep_rate[:, NP + q : NP + q + 1])
+            nc.scalar.activation(u_t[q][:], z_t[q][:], COPY, scale=stay[:, along + q : along + q + 1])
 
         def product_turned(q):
-            eq[q] = psum.tile([P, 512], F32, name="acc")
-            nc.tensor.matmul_mx(
-                out=eq[q][:],
-                lhsT=zq[q][0].bitcast(FP8X4),
-                lhsT_scale=zq[q][1],
-                rhs=w2q[0][:].bitcast(FP8X4),
-                rhs_scale=w2q[1][:],
-                start=True,
-                stop=True,
-            )
+            eq[q] = bank()
+            product(eq[q][:], zq[q], (w2q[0][:], w2q[1][:]))
 
         def product_planes(q):
-            eq[q] = psum.tile([P, 512], F32, name="acc")
+            eq[q] = bank()
             for t in range(4):
-                nc.tensor.matmul_mx(
-                    out=eq[q][:, P * t : P * t + P],
-                    lhsT=w2q[0][:, P * t : P * t + P].bitcast(FP8X4),
-                    lhsT_scale=w2q[1][:, P * t : P * t + P],
-                    rhs=zq[q][0].bitcast(FP8X4),
-                    rhs_scale=zq[q][1],
-                    start=True,
-                    stop=True,
-                )
+                product(eq[q][:, P * t : P * t + P], columns(w2q, P * t, P), zq[q])
 
         def relax_turned(q):
             o_t[q] = on_vector([P, 512], F32, f"o_t{q}")
-            nc.vector.scalar_tensor_tensor(o_t[q][:], eq[q][:], rate[:, NP + q : NP + q + 1], u_t[q][:], MULT, ADD)
+            nc.vector.scalar_tensor_tensor(o_t[q][:], eq[q][:], rate[:, along + q : along + q + 1], u_t[q][:], MULT, ADD)
 
         def turn_back(q):
-            back[q] = psum.tile([P, 512], F32, name="acc")
+            back[q] = bank()
             for t in range(4):
                 nc.tensor.transpose(back[q][:, P * t : P * t + P], o_t[q][:, P * t : P * t + P], ident[:])
 
@@ -219,9 +208,13 @@ def tile_picked_lbm8_none_po_kernel(
             nc.scalar.copy(outs[q][:], planes(back[q]))
             store(q)
 
-        def kept_planes(q):
+        def kept_on_gpsimd(q):
             kept[q] = planes(work[q])
-            nc.gpsimd.tensor_tensor(kept[q], z[q], along_cells(keep_rate, q), MULT)
+            nc.gpsimd.tensor_tensor(kept[q], z[q], along_cells(stay, q), MULT)
+
+        def kept_on_vector(q):
+            kept[q] = on_vector([P, 4, P], F32, f"kept{q}")[:]
+            nc.vector.tensor_tensor(kept[q], z[q], along_cells(stay, q), MULT)
 
         def moved_planes(q):
             moved[q] = on_vector([P, 4, P], F32, f"moved{q}")
@@ -232,83 +225,78 @@ def tile_picked_lbm8_none_po_kernel(
             nc.vector.tensor_tensor(outs[q][:], moved[q][:], kept[q], ADD)
             store(q)
 
-        def round_out(engine_copy, q):
+        def round_turned(q):
+            ob[q] = on_scalar([P, P, 4], BF16, f"ob{q}")
+            nc.scalar.copy(ob[q][:], planes(back[q]).rearrange("p t c -> p c t"))
+
+        def round_planes(engine_copy, make, q):
+            ob[q] = make([P, P, 4], BF16, f"ob{q}")
+            interleave(engine_copy, ob[q][:], outs[q][:])
+
+        def quantise_out(q):
             h, e = divmod(q, 2)
             if e == 0:
-                ob[h] = on_scalar([P, 2 * P, 4], BF16, f"ob{h}")
-            if q < TURNED:
-                engine_copy(ob[h][:, P * e : P * e + P, :], planes(back[q]).rearrange("p t c -> p c t"))
-            else:
-                interleave(engine_copy, ob[h][:, P * e : P * e + P, :], outs[q][:])
-
-        def quant_out(first, count):
-            h, e = divmod(first, 2)
-            if e == 0:
-                o_codes[h] = on_vector([P, 2 * P], I32, f"o_codes{h}")
-            nc.vector.quantize_mx(
-                out=o_codes[h][:, P * e : P * (e + count)].bitcast(FP8X4),
-                scales=o_scales[:, P * first : P * (first + count)],
-                in_=ob[h][:, P * e : P * (e + count), :].rearrange("p n t -> p (n t)"),
+                o_codes[h] = on_vector([P, HALF], I32, f"o_codes{h}")
+            quantise(
+                o_codes[h][:, P * e : P * e + P], o_scales[:, P * q : P * q + P], ob[q][:].rearrange("p n t -> p (n t)")
             )
-            if e + count == 2:
-                nc.sync.dma_start(out1_v[:, 2 * P * h : 2 * P * h + 2 * P], o_codes[h][:])
+            if e == 1:
+                nc.sync.dma_start(out1_v[:, HALF * h : HALF * h + HALF], o_codes[h][:])
 
-        vector_copy = nc.vector.tensor_copy
-        z01 = on_vector([P, 4, 2 * P], F32, "z01")
+        z01 = on_vector([P, 4, HALF], F32, "z01")
+        z[0], z[1] = z01[:, :, 0:P], z01[:, :, P:HALF]
         for t in range(3):
             gather(vector_copy, z01, t, 0, 2)
-        for q in range(2):
-            gather(vector_copy, z01[:, :, P * q : P * q + P], 3, q, 1)
-        z[0], z[1] = z01[:, :, 0:P], z01[:, :, P : 2 * P]
-        for t in (1, 2, 3):
-            gather(scalar_copy, z2, t, 2, 1)
-        z[2] = z2[:]
+        gather(vector_copy, z[0], 3, 0, 1)
+        z[2] = on_scalar([P, 4, P], F32, "z2")[:]
+        gather(scalar_copy, z[2], 0, 2, 1)
+        gather(scalar_copy, z[1], 3, 1, 1)
+        gather(scalar_copy, z[2], 1, 2, 1)
+        gather(scalar_copy, z[2], 2, 2, 1)
+        stay = on_scalar([P, along + TURNED], F32, "stay")
+        nc.scalar.activation(stay[:], rate[:], COPY, scale=-1.0, bias=1.0)
+        gather(scalar_copy, z[2], 3, 2, 1)
+        quantise_w2(1)
         round_z(vector_copy, on_vector, 0)
-        round_z(nc.scalar.copy, on_scalar, 1)
-        w2q[0], w2q[1] = quant(w2g[:].rearrange("p t m j -> p (t m j)"), H, "w2q")
-        keep_rate = on_vector([P, NP + TURNED], F32, "keep_rate")
-        nc.vector.tensor_scalar(keep_rate[:], rate[:], -1.0, 1.0, MULT, ADD)
+        round_z(vector_copy, on_vector, 1)
         turn_z(0)
         turn_z(1)
-        z[3] = planes(work[1])
-        gather(scalar_copy, z[3], 2, 3, 1)
-        gather(scalar_copy, z[3], 3, 3, 1)
-        quant_z(0)
-        round_z(vector_copy, on_vector, 2)
-        quant_z(1)
+        quantise_z(0)
+        quantise_z(1)
         kept_turned(0)
+        kept_turned(1)
         product_turned(0)
         product_turned(1)
-        kept_turned(1)
-        quant_z(2)
+        round_z(vector_copy, on_vector, 2)
+        z[3] = on_vector([P, 4, P], F32, "z3")[:]
         gather(vector_copy, z[3], 0, 3, 1)
+        quantise_z(2)
         gather(vector_copy, z[3], 1, 3, 1)
-        kept_planes(2)
-        round_z(nc.scalar.copy, on_scalar, 3)
+        gather(scalar_copy, z[3], 2, 3, 1)
+        gather(scalar_copy, z[3], 3, 3, 1)
+        kept_on_gpsimd(2)
         product_planes(2)
+        round_z(nc.scalar.copy, on_scalar, 3)
         relax_turned(0)
         relax_turned(1)
         turn_back(0)
         turn_back(1)
-        quant_z(3)
+        moved_planes(2)
+        quantise_z(3)
         product_planes(3)
         leave_psum(0)
-        leave_psum(1)
-        moved_planes(2)
-        kept3 = on_vector([P, 4, P], F32, "kept3")
-        kept[3] = kept3[:]
-        nc.vector.tensor_tensor(kept[3], z[3], along_cells(keep_rate, 3), MULT)
-        moved_planes(3)
-        round_out(nc.scalar.copy, 0)
-        round_out(nc.scalar.copy, 1)
         relax_planes(2)
+        leave_psum(1)
+        kept_on_vector(3)
+        moved_planes(3)
+        round_turned(0)
+        round_turned(1)
+        quantise_out(0)
         relax_planes(3)
-        round_out(nc.scalar.copy, 2)
-        quant_out(0, 2)
-        round_out(vector_copy, 3)
-        quant_out(2, 1)
-        quant_out(3, 1)
-        for q in range(4):
-            (nc.scalar, nc.sync)[q % 2].dma_start(
-                out_2[0, q:16:4, :].bitcast(I32), o_scales[q:P:32, :].bitcast(I32)
-            )
+        quantise_out(1)
+        round_planes(nc.scalar.copy, on_scalar, 2)
+        round_planes(vector_copy, on_vector, 3)
+        quantise_out(2)
+        quantise_out(3)
+        for r in range(4):
+            (nc.scalar, nc.sync)[r % 2].dma_start(out_2[0, r:16:4, :].bitcast(I32), o_scales[r:P:32, :].bitcast(I32))

@@ -70,14 +70,14 @@ def tile_picked_lbm8_none_po_kernel(
         xs = keep.tile([P, T], U8, name="xs")
         ident = keep.tile([P, P], F32, name="ident")
 
-        w1_raw = [keep.tile([P, 4, HALF], F32, name=f"w1_raw{h}") for h in range(2)]
+        w1_raw = [keep.tile([P, 2, H], F32, name=f"w1_raw{h}") for h in range(2)]
         nc.vector.memset(xs[:].bitcast(I32), 0)
         w1_rows = w1.rearrange("(p j) c -> p j c", j=4)
-        nc.sync.dma_start(w1_raw[0][:], w1_rows[:, :, 0:HALF])
+        nc.sync.dma_start(w1_raw[0][:], w1_rows[:, 0:2, :])
         nc.sync.dma_start(offs_t[:], offs)
         for r in range(4):
             nc.sync.dma_start(xs[r:P:32, :].bitcast(I32), x_scales[0, r:16:4, :].bitcast(I32))
-        nc.sync.dma_start(w1_raw[1][:], w1_rows[:, :, HALF:H])
+        nc.sync.dma_start(w1_raw[1][:], w1_rows[:, 2:4, :])
         nc.sync.dma_start(xw[:], x_words[0].rearrange("p n t -> p (n t)").bitcast(I32))
         nc.sync.dma_start(stream_t[:], stream)
         w2_rows = w2.rearrange("(p j) c -> p j c", j=4)
@@ -94,7 +94,7 @@ def tile_picked_lbm8_none_po_kernel(
 
         def round_w1(engine_copy, u, h):
             engine_copy(
-                w1g[u][:, :, 64 * h : 64 * h + 64, :].rearrange("p t m j -> p m j t"),
+                w1g[u][:, :, :, 2 * h : 2 * h + 2].rearrange("p t m j -> p m j t"),
                 w1_raw[h][:].rearrange("p j (m t) -> p m j t", t=4)[:, :, :, 2 * u : 2 * u + 2],
             )
 

@@ -19,6 +19,8 @@ K, T, S, H = 512, 2048, 512, 512
 FLOPS = 2 * 2 * 512 * 512 * 512
 HALF = 256
 TURNED = 2
+LEAD = 8
+SUBTRACT = mybir.AluOpType.subtract
 
 
 def tile_picked_lbm8_none_po_kernel(
@@ -31,7 +33,7 @@ def tile_picked_lbm8_none_po_kernel(
         psum = ctx.enter_context(tc.psum_pool(name="psum", bufs=8))
 
         def on_vector(shape, dtype, name):
-            return queue.tile(shape, dtype, name=name, tag="vector", bufs=30, align_bytes=64)
+            return queue.tile(shape, dtype, name=name, tag="vector", bufs=34, align_bytes=64)
 
         def on_scalar(shape, dtype, name):
             return queue.tile(shape, dtype, name=name, tag="scalar", bufs=20, align_bytes=64)
@@ -86,10 +88,10 @@ def tile_picked_lbm8_none_po_kernel(
         for i, (a, n) in enumerate(w2_cuts):
             nc.sync.dma_start(w2_raw[i][:], w2_rows[:, :, a : a + n])
         along = S - P * TURNED
-        rate = keep.tile([P, along + TURNED], F32, name="rate")
-        nc.sync.dma_start(rate[:, 0:along], om[:, P * TURNED : S])
+        rate = keep.tile([P, LEAD + along], F32, name="rate")
+        nc.sync.dma_start(rate[:, LEAD:], om[:, P * TURNED : S])
         with nc.allow_non_contiguous_dma(reason="one rate for each partition"):
-            nc.sync.dma_start(rate[:, along : along + TURNED], om[0, 0 : P * TURNED].rearrange("(q p) -> p q", p=P))
+            nc.sync.dma_start(rate[:, LEAD - TURNED : LEAD], om[0, 0 : P * TURNED].rearrange("(q p) -> p q", p=P))
         make_identity(nc, ident[:])
 
         def round_w1(engine_copy, u, h):
@@ -155,7 +157,7 @@ def tile_picked_lbm8_none_po_kernel(
             return tile[:].rearrange("p (t j) -> p t j", t=4)
 
         def along_cells(row, q):
-            first = (q - TURNED) * P
+            first = LEAD + (q - TURNED) * P
             return row[:, first : first + P].unsqueeze(1).to_broadcast([P, 4, P])
 
         def interleave(engine_copy, dst, src):
@@ -180,7 +182,7 @@ def tile_picked_lbm8_none_po_kernel(
 
         def kept_turned(q):
             u_t[q] = on_scalar([P, 512], F32, f"u_t{q}")
-            nc.scalar.activation(u_t[q][:], z_t[q][:], COPY, scale=stay[:, along + q : along + q + 1])
+            nc.scalar.activation(u_t[q][:], z_t[q][:], COPY, scale=stay[:, LEAD - TURNED + q : LEAD - TURNED + q + 1])
 
         def product_turned(q):
             eq[q] = bank()
@@ -193,7 +195,7 @@ def tile_picked_lbm8_none_po_kernel(
 
         def relax_turned(q):
             o_t[q] = on_vector([P, 512], F32, f"o_t{q}")
-            nc.vector.scalar_tensor_tensor(o_t[q][:], eq[q][:], rate[:, along + q : along + q + 1], u_t[q][:], MULT, ADD)
+            nc.vector.scalar_tensor_tensor(o_t[q][:], eq[q][:], rate[:, LEAD - TURNED + q : LEAD - TURNED + q + 1], u_t[q][:], MULT, ADD)
 
         def turn_back(q):
             back[q] = bank()
@@ -214,7 +216,7 @@ def tile_picked_lbm8_none_po_kernel(
 
         def kept_on_vector(q):
             kept[q] = on_vector([P, 4, P], F32, f"kept{q}")[:]
-            nc.vector.tensor_tensor(kept[q], z[q], along_cells(stay, q), MULT)
+            nc.vector.scalar_tensor_tensor(kept[q], along_cells(rate, q), 1.0, z[q], SUBTRACT, MULT)
 
         def moved_planes(q):
             moved[q] = on_vector([P, 4, P], F32, f"moved{q}")
@@ -233,15 +235,13 @@ def tile_picked_lbm8_none_po_kernel(
             ob[q] = make([P, P, 4], BF16, f"ob{q}")
             interleave(engine_copy, ob[q][:], outs[q][:])
 
-        def quantise_out(q):
-            h, e = divmod(q, 2)
-            if e == 0:
-                o_codes[h] = on_vector([P, HALF], I32, f"o_codes{h}")
-            quantise(
-                o_codes[h][:, P * e : P * e + P], o_scales[:, P * q : P * q + P], ob[q][:].rearrange("p n t -> p (n t)")
-            )
-            if e == 1:
-                nc.sync.dma_start(out1_v[:, HALF * h : HALF * h + HALF], o_codes[h][:])
+        def quantise_out(q, first, last):
+            if q == first:
+                o_codes[first] = on_vector([P, P * (last + 1 - first)], I32, f"o_codes{first}")
+            at = P * (q - first)
+            quantise(o_codes[first][:, at : at + P], o_scales[:, P * q : P * q + P], ob[q][:].rearrange("p n t -> p (n t)"))
+            if q == last:
+                nc.sync.dma_start(out1_v[:, P * first : P * last + P], o_codes[first][:])
 
         z01 = on_vector([P, 4, HALF], F32, "z01")
         z[0], z[1] = z01[:, :, 0:P], z01[:, :, P:HALF]
@@ -253,8 +253,8 @@ def tile_picked_lbm8_none_po_kernel(
         gather(scalar_copy, z[1], 3, 1, 1)
         gather(scalar_copy, z[2], 1, 2, 1)
         gather(scalar_copy, z[2], 2, 2, 1)
-        stay = on_scalar([P, along + TURNED], F32, "stay")
-        nc.scalar.activation(stay[:], rate[:], COPY, scale=-1.0, bias=1.0)
+        stay = on_scalar([P, LEAD + P], F32, "stay")
+        nc.scalar.activation(stay[:, LEAD - TURNED :], rate[:, LEAD - TURNED : LEAD + P], COPY, scale=-1.0, bias=1.0)
         gather(scalar_copy, z[2], 3, 2, 1)
         quantise_w2(1)
         round_z(vector_copy, on_vector, 0)
@@ -271,13 +271,13 @@ def tile_picked_lbm8_none_po_kernel(
         z[3] = on_vector([P, 4, P], F32, "z3")[:]
         gather(vector_copy, z[3], 0, 3, 1)
         quantise_z(2)
-        gather(vector_copy, z[3], 1, 3, 1)
         gather(scalar_copy, z[3], 2, 3, 1)
         gather(scalar_copy, z[3], 3, 3, 1)
         kept_on_gpsimd(2)
         product_planes(2)
-        round_z(nc.scalar.copy, on_scalar, 3)
         relax_turned(0)
+        gather(vector_copy, z[3], 1, 3, 1)
+        round_z(nc.scalar.copy, on_scalar, 3)
         relax_turned(1)
         turn_back(0)
         turn_back(1)
@@ -288,15 +288,23 @@ def tile_picked_lbm8_none_po_kernel(
         relax_planes(2)
         leave_psum(1)
         kept_on_vector(3)
-        moved_planes(3)
         round_turned(0)
         round_turned(1)
-        quantise_out(0)
-        relax_planes(3)
-        quantise_out(1)
         round_planes(nc.scalar.copy, on_scalar, 2)
-        round_planes(vector_copy, on_vector, 3)
-        quantise_out(2)
-        quantise_out(3)
+        halves = [slice(64 * e, 64 * e + 64) for e in range(2)]
+        moved3 = [on_vector([P, 4, 64], F32, f"moved3{e}") for e in range(2)]
+        for e in range(2):
+            nc.vector.tensor_tensor(moved3[e][:], planes(eq[3])[:, :, halves[e]], along_cells(rate, 3)[:, :, halves[e]], MULT)
+        outs[3] = on_vector([P, 4, P], F32, "o3")
+        for e in range(2):
+            nc.vector.tensor_tensor(outs[3][:, :, halves[e]], moved3[e][:], kept[3][:, :, halves[e]], SUBTRACT)
+        store(3)
+        quantise_out(0, 0, 1)
+        ob[3] = on_vector([P, P, 4], BF16, "ob3")
+        interleave(vector_copy, ob[3][:, halves[0], :], outs[3][:, :, halves[0]])
+        quantise_out(1, 0, 1)
+        interleave(vector_copy, ob[3][:, halves[1], :], outs[3][:, :, halves[1]])
+        quantise_out(2, 2, 3)
+        quantise_out(3, 2, 3)
         for r in range(4):
             (nc.scalar, nc.sync)[r % 2].dma_start(out_2[0, r:16:4, :].bitcast(I32), o_scales[r:P:32, :].bitcast(I32))

@@ -279,16 +279,21 @@ def tile_picked_lbm8_none_po_kernel(
         gather(vector_copy, z[3], 1, 3, 1)
         round_z(nc.scalar.copy, on_scalar, 3)
         relax_turned(1)
-        turn_back(0)
+        pairs0 = [bank() for e in range(2)]
+        for t in range(4):
+            nc.tensor.transpose(pairs0[t // 2][:, P * (t % 2) : P * (t % 2) + P], o_t[0][:, P * t : P * t + P], ident[:])
         turn_back(1)
         moved_planes(2)
         quantise_z(3)
         product_planes(3)
-        leave_psum(0)
+        outs[0] = on_scalar([P, 4, P], F32, "o0")
+        for e in range(2):
+            nc.scalar.copy(outs[0][:, 2 * e : 2 * e + 2, :], pairs0[e][:, 0:HALF].rearrange("p (t j) -> p t j", t=2))
+        store(0)
         relax_planes(2)
         leave_psum(1)
         kept_on_vector(3)
-        round_turned(0)
+        round_planes(nc.scalar.copy, on_scalar, 0)
         round_turned(1)
         round_planes(nc.scalar.copy, on_scalar, 2)
         halves = [slice(64 * e, 64 * e + 64) for e in range(2)]

@@ -198,17 +198,13 @@ def tile_picked_lbm8_none_po_kernel(
             nc.vector.scalar_tensor_tensor(o_t[q][:], eq[q][:], rate[:, LEAD - TURNED + q : LEAD - TURNED + q + 1], u_t[q][:], MULT, ADD)
 
         def turn_back(q):
-            back[q] = bank()
+            back[q] = [bank() for e in range(2)]
             for t in range(4):
-                nc.tensor.transpose(back[q][:, P * t : P * t + P], o_t[q][:, P * t : P * t + P], ident[:])
-
-        def store(q):
-            nc.sync.dma_start(out0_v[:, :, q * P : q * P + P], outs[q][:])
+                nc.tensor.transpose(back[q][t // 2][:, P * (t % 2) : P * (t % 2) + P], o_t[q][:, P * t : P * t + P], ident[:])
 
         def leave_psum(q):
-            outs[q] = on_scalar([P, 4, P], F32, f"o{q}")
-            nc.scalar.copy(outs[q][:], planes(back[q]))
-            store(q)
+            for e in range(2):
+                nc.scalar.copy(outs[q][:, 2 * e : 2 * e + 2, :], back[q][e][:, 0:HALF].rearrange("p (t j) -> p t j", t=2))
 
         def kept_on_gpsimd(q):
             kept[q] = planes(work[q])
@@ -222,18 +218,9 @@ def tile_picked_lbm8_none_po_kernel(
             moved[q] = on_vector([P, 4, P], F32, f"moved{q}")
             nc.vector.tensor_tensor(moved[q][:], planes(eq[q]), along_cells(rate, q), MULT)
 
-        def relax_planes(q):
-            outs[q] = on_vector([P, 4, P], F32, f"o{q}")
-            nc.vector.tensor_tensor(outs[q][:], moved[q][:], kept[q], ADD)
-            store(q)
-
-        def round_turned(q):
-            ob[q] = on_scalar([P, P, 4], BF16, f"ob{q}")
-            nc.scalar.copy(ob[q][:], planes(back[q]).rearrange("p t c -> p c t"))
-
         def round_planes(engine_copy, make, q):
             ob[q] = make([P, P, 4], BF16, f"ob{q}")
-            interleave(engine_copy, ob[q][:], outs[q][:])
+            interleave(engine_copy, ob[q][:], outs[q])
 
         def quantise_out(q, first, last):
             if q == first:
@@ -279,23 +266,23 @@ def tile_picked_lbm8_none_po_kernel(
         gather(vector_copy, z[3], 1, 3, 1)
         round_z(nc.scalar.copy, on_scalar, 3)
         relax_turned(1)
-        pairs0 = [bank() for e in range(2)]
-        for t in range(4):
-            nc.tensor.transpose(pairs0[t // 2][:, P * (t % 2) : P * (t % 2) + P], o_t[0][:, P * t : P * t + P], ident[:])
+        turn_back(0)
         turn_back(1)
         moved_planes(2)
         quantise_z(3)
         product_planes(3)
-        outs[0] = on_scalar([P, 4, P], F32, "o0")
+        outs[0] = on_scalar([P, 4, P], F32, "o0")[:]
+        leave_psum(0)
         for e in range(2):
-            nc.scalar.copy(outs[0][:, 2 * e : 2 * e + 2, :], pairs0[e][:, 0:HALF].rearrange("p (t j) -> p t j", t=2))
-        store(0)
-        relax_planes(2)
+            nc.sync.dma_start(out0_v[:, 2 * e : 2 * e + 2, 0:P], outs[0][:, 2 * e : 2 * e + 2, :])
+        o12 = on_vector([P, 4, HALF], F32, "o12")
+        outs[1], outs[2] = o12[:, :, 0:P], o12[:, :, P:HALF]
+        nc.vector.tensor_tensor(outs[2], moved[2][:], kept[2], ADD)
         leave_psum(1)
+        nc.sync.dma_start(out0_v[:, :, P : P + HALF], o12[:])
         kept_on_vector(3)
-        round_planes(nc.scalar.copy, on_scalar, 0)
-        round_turned(1)
-        round_planes(nc.scalar.copy, on_scalar, 2)
+        for q in range(3):
+            round_planes(nc.scalar.copy, on_scalar, q)
         halves = [slice(64 * e, 64 * e + 64) for e in range(2)]
         moved3 = [on_vector([P, 4, 64], F32, f"moved3{e}") for e in range(2)]
         for e in range(2):
@@ -303,7 +290,7 @@ def tile_picked_lbm8_none_po_kernel(
         outs[3] = on_vector([P, 4, P], F32, "o3")
         for e in range(2):
             nc.vector.tensor_tensor(outs[3][:, :, halves[e]], moved3[e][:], kept[3][:, :, halves[e]], SUBTRACT)
-        store(3)
+        nc.sync.dma_start(out0_v[:, :, 3 * P : S], outs[3][:])
         quantise_out(0, 0, 1)
         ob[3] = on_vector([P, P, 4], BF16, "ob3")
         interleave(vector_copy, ob[3][:, halves[0], :], outs[3][:, :, halves[0]])

@@ -139,13 +139,13 @@ def tile_picked_lbm8_none_po_kernel(
 
         w2q = (keep.tile([P, H], U32, name="w2_codes", align_bytes=64), keep.tile([P, H], U8, name="w2_scales", align_bytes=64))
 
-        def quantise_w2(h):
-            for t in range(4):
+        def quantise_w2(h, planes_wanted):
+            for t in planes_wanted:
                 quantise(*columns(w2q, P * t + 64 * h, 64), w2g[h][:, t, :, :].rearrange("p m j -> p (m j)"))
 
         round_w2(vector_copy, 0, "p m j t")
         round_w2(vector_copy, 1, "p m j t")
-        quantise_w2(0)
+        quantise_w2(0, range(4))
         round_w2(gpsimd_copy, 2, "p t m j")
 
         o_scales = keep.tile([P, S], U8, name="o_scales", align_bytes=64)
@@ -210,10 +210,6 @@ def tile_picked_lbm8_none_po_kernel(
             kept[q] = planes(work[q])
             nc.gpsimd.tensor_tensor(kept[q], z[q], along_cells(stay, q), MULT)
 
-        def kept_on_vector(q):
-            kept[q] = on_vector([P, 4, P], F32, f"kept{q}")[:]
-            nc.vector.scalar_tensor_tensor(kept[q], along_cells(rate, q), 1.0, z[q], SUBTRACT, MULT)
-
         def moved_planes(q):
             moved[q] = on_vector([P, 4, P], F32, f"moved{q}")
             nc.vector.tensor_tensor(moved[q][:], planes(eq[q]), along_cells(rate, q), MULT)
@@ -243,12 +239,13 @@ def tile_picked_lbm8_none_po_kernel(
         stay = on_scalar([P, LEAD + P], F32, "stay")
         nc.scalar.activation(stay[:, LEAD - TURNED :], rate[:, LEAD - TURNED : LEAD + P], COPY, scale=-1.0, bias=1.0)
         gather(scalar_copy, z[2], 3, 2, 1)
-        quantise_w2(1)
+        quantise_w2(1, range(3))
         round_z(vector_copy, on_vector, 0)
         round_z(vector_copy, on_vector, 1)
         turn_z(0)
         turn_z(1)
         quantise_z(0)
+        quantise_w2(1, range(3, 4))
         quantise_z(1)
         kept_turned(0)
         kept_turned(1)
@@ -270,7 +267,16 @@ def tile_picked_lbm8_none_po_kernel(
         turn_back(1)
         moved_planes(2)
         quantise_z(3)
-        product_planes(3)
+        pairs = [slice(2 * e, 2 * e + 2) for e in range(2)]
+        eq3 = [bank() for e in range(2)]
+        for t in range(4):
+            product(eq3[t // 2][:, P * (t % 2) : P * (t % 2) + P], columns(w2q, P * t, P), zq[3])
+
+        def lost_pair(e):
+            kept[3, e] = on_vector([P, 2, P], F32, f"lost3{e}")
+            nc.vector.scalar_tensor_tensor(kept[3, e][:], along_cells(rate, 3)[:, pairs[e], :], 1.0, z[3][:, pairs[e], :], SUBTRACT, MULT)
+
+        lost_pair(0)
         outs[0] = on_scalar([P, 4, P], F32, "o0")[:]
         leave_psum(0)
         for e in range(2):
@@ -280,22 +286,20 @@ def tile_picked_lbm8_none_po_kernel(
         nc.vector.tensor_tensor(outs[2], moved[2][:], kept[2], ADD)
         leave_psum(1)
         nc.sync.dma_start(out0_v[:, :, P : P + HALF], o12[:])
-        kept_on_vector(3)
+        lost_pair(1)
         for q in range(3):
             round_planes(nc.scalar.copy, on_scalar, q)
-        halves = [slice(64 * e, 64 * e + 64) for e in range(2)]
-        moved3 = [on_vector([P, 4, 64], F32, f"moved3{e}") for e in range(2)]
+        moved3 = [on_vector([P, 2, P], F32, f"moved3{e}") for e in range(2)]
         for e in range(2):
-            nc.vector.tensor_tensor(moved3[e][:], planes(eq[3])[:, :, halves[e]], along_cells(rate, 3)[:, :, halves[e]], MULT)
-        outs[3] = on_vector([P, 4, P], F32, "o3")
+            pair = eq3[e][:, 0:HALF].rearrange("p (t j) -> p t j", t=2)
+            nc.vector.tensor_tensor(moved3[e][:], pair, along_cells(rate, 3)[:, pairs[e], :], MULT)
+        outs[3] = on_vector([P, 4, P], F32, "o3")[:]
         for e in range(2):
-            nc.vector.tensor_tensor(outs[3][:, :, halves[e]], moved3[e][:], kept[3][:, :, halves[e]], SUBTRACT)
-        nc.sync.dma_start(out0_v[:, :, 3 * P : S], outs[3][:])
+            nc.vector.tensor_tensor(outs[3][:, pairs[e], :], moved3[e][:], kept[3, e][:], SUBTRACT)
+        nc.sync.dma_start(out0_v[:, :, 3 * P : S], outs[3])
         quantise_out(0, 0, 1)
-        ob[3] = on_vector([P, P, 4], BF16, "ob3")
-        interleave(vector_copy, ob[3][:, halves[0], :], outs[3][:, :, halves[0]])
         quantise_out(1, 0, 1)
-        interleave(vector_copy, ob[3][:, halves[1], :], outs[3][:, :, halves[1]])
+        round_planes(vector_copy, on_vector, 3)
         quantise_out(2, 2, 3)
         quantise_out(3, 2, 3)
         for r in range(4):

@@ -194,13 +194,17 @@ def tile_picked_lbm8_none_po_kernel(
                 product(eq[q][:, P * t : P * t + P], columns(w2q, P * t, P), zq[q])
 
         def relax_turned(q):
-            o_t[q] = on_vector([P, 512], F32, f"o_t{q}")
-            nc.vector.scalar_tensor_tensor(o_t[q][:], eq[q][:], rate[:, LEAD - TURNED + q : LEAD - TURNED + q + 1], u_t[q][:], MULT, ADD)
+            o_t[q] = [on_vector([P, HALF], F32, f"o_t{q}{e}") for e in range(2)]
+            for e in range(2):
+                cols = slice(HALF * e, HALF * e + HALF)
+                nc.vector.scalar_tensor_tensor(
+                    o_t[q][e][:], eq[q][:, cols], rate[:, LEAD - TURNED + q : LEAD - TURNED + q + 1], u_t[q][:, cols], MULT, ADD
+                )
 
         def turn_back(q):
             back[q] = [bank() for e in range(2)]
             for t in range(4):
-                nc.tensor.transpose(back[q][t // 2][:, P * (t % 2) : P * (t % 2) + P], o_t[q][:, P * t : P * t + P], ident[:])
+                nc.tensor.transpose(back[q][t // 2][:, P * (t % 2) : P * (t % 2) + P], o_t[q][t // 2][:, P * (t % 2) : P * (t % 2) + P], ident[:])
 
         def leave_psum(q):
             for e in range(2):

from contextlib import ExitStack

import concourse.mybir as mybir
from concourse.masks import make_identity

F32 = mybir.dt.float32
BF16 = mybir.dt.bfloat16
I32 = mybir.dt.int32
U32 = mybir.dt.uint32
U16 = mybir.dt.uint16
U8 = mybir.dt.uint8
FP8X4 = mybir.dt.float8_e4m3fn_x4
MULT = mybir.AluOpType.mult
ADD = mybir.AluOpType.add
COPY = mybir.ActivationFunctionType.Copy

P = 128
K, T, S, H = 512, 2048, 512, 512
FLOPS = 2 * 2 * 512 * 512 * 512
HALF = 256
TURNED = 2
LEAD = 8
SUBTRACT = mybir.AluOpType.subtract


def tile_picked_lbm8_none_po_kernel(
    tc, x_words, x_scales, w1, w2, om, offs, stream, out_0, out_1, out_2
):
    nc = tc.nc
    with ExitStack() as ctx:
        keep = ctx.enter_context(tc.tile_pool(name="keep", bufs=1))
        queue = ctx.enter_context(tc.tile_pool(name="queue", bufs=1))
        psum = ctx.enter_context(tc.psum_pool(name="psum", bufs=8))

        def on_vector(shape, dtype, name):
            return queue.tile(shape, dtype, name=name, tag="vector", bufs=34, align_bytes=64)

        def on_scalar(shape, dtype, name):
            return queue.tile(shape, dtype, name=name, tag="scalar", bufs=20, align_bytes=64)

        def bank():
            return psum.tile([P, 512], F32, name="bank")

        vector_copy = nc.vector.tensor_copy

        def scalar_copy(dst, src):
            nc.scalar.activation(dst, src, COPY)

        def gpsimd_copy(dst, src):
            nc.gpsimd.tensor_scalar(dst, src, 1.0, 0.0, MULT, ADD)

        def quantise(codes, scales, values):
            nc.vector.quantize_mx(out=codes.bitcast(FP8X4), scales=scales, in_=values)

        def product(out, still, moving):
            nc.tensor.matmul_mx(
                out=out,
                lhsT=still[0].bitcast(FP8X4),
                lhsT_scale=still[1],
                rhs=moving[0].bitcast(FP8X4),
                rhs_scale=moving[1],
                start=True,
                stop=True,
            )

        def columns(pair, first, count):
            return pair[0][:, first : first + count], pair[1][:, first : first + count]

        offs_t = keep.tile([P, S // 16], U16, name="offs_t")
        stream_t = keep.tile([P, S // 16], U16, name="stream_t")
        xw = keep.tile([P, T], I32, name="xw")
        xs = keep.tile([P, T], U8, name="xs")
        ident = keep.tile([P, P], F32, name="ident")

        w1_raw = [keep.tile([P, 2, H], F32, name=f"w1_raw{h}") for h in range(2)]
        nc.vector.memset(xs[:].bitcast(I32), 0)
        w1_rows = w1.rearrange("(p j) c -> p j c", j=4)
        nc.sync.dma_start(w1_raw[0][:], w1_rows[:, 0:2, :])
        nc.sync.dma_start(offs_t[:], offs)
        for r in range(4):
            nc.sync.dma_start(xs[r:P:32, :].bitcast(I32), x_scales[0, r:16:4, :].bitcast(I32))
        nc.sync.dma_start(w1_raw[1][:], w1_rows[:, 2:4, :])
        nc.sync.dma_start(xw[:], x_words[0].rearrange("p n t -> p (n t)").bitcast(I32))
        nc.sync.dma_start(stream_t[:], stream)
        w2_rows = w2.rearrange("(p j) c -> p j c", j=4)
        w2_cuts = ((0, HALF), (HALF, P), (HALF + P, P))
        w2_raw = [keep.tile([P, 4, n], F32, name=f"w2_raw{i}") for i, (a, n) in enumerate(w2_cuts)]
        for i, (a, n) in enumerate(w2_cuts):
            nc.sync.dma_start(w2_raw[i][:], w2_rows[:, :, a : a + n])
        along = S - P * TURNED
        rate = keep.tile([P, LEAD + along], F32, name="rate")
        nc.sync.dma_start(rate[:, LEAD:], om[:, P * TURNED : S])
        with nc.allow_non_contiguous_dma(reason="one rate for each partition"):
            nc.sync.dma_start(rate[:, LEAD - TURNED : LEAD], om[0, 0 : P * TURNED].rearrange("(q p) -> p q", p=P))
        make_identity(nc, ident[:])

        def round_w1(engine_copy, u, h):
            engine_copy(
                w1g[u][:, :, :, 2 * h : 2 * h + 2].rearrange("p t m j -> p m j t"),
                w1_raw[h][:].rearrange("p j (m t) -> p m j t", t=4)[:, :, :, 2 * u : 2 * u + 2],
            )

        def quantise_w1(grouped, u):
            pair = (on_vector([P, HALF], U32, f"w1_codes{u}"), keep.tile([P, HALF], U8, name=f"w1_scales{u}", align_bytes=64))
            quantise(pair[0][:], pair[1][:], grouped[:].rearrange("p t m j -> p (t m j)"))
            return pair

        w1g = [on_vector([P, 2, P, 4], BF16, "w1g0"), on_scalar([P, 2, P, 4], BF16, "w1g1")]
        round_w1(vector_copy, 0, 0)
        round_w1(scalar_copy, 1, 0)
        xg_scales = on_vector([P, S], U8, "xg_scales")
        vector_copy(xg_scales[:], xs[:].indirect(offs_t[:]))
        round_w1(vector_copy, 0, 1)
        round_w1(scalar_copy, 1, 1)
        w1q = [quantise_w1(w1g[u], u) for u in range(2)]
        xq = []
        for h in range(2):
            words = on_vector([P, HALF], U32, f"xg_words{h}")
            vector_copy(words[:], xw[:].bitcast(U32).indirect(offs_t[:, 16 * h : 16 * h + 16]))
            xq.append((words[:], xg_scales[:, HALF * h : HALF * h + HALF]))

        y = {}
        for t, h in ((0, 0), (1, 0), (0, 1), (1, 1), (2, 0), (2, 1), (3, 0), (3, 1)):
            if h == 0:
                y[t] = on_scalar([P, S], F32, f"y{t}")
            acc = bank()
            product(acc[:, 0:HALF], columns(w1q[t // 2], P * (t % 2), P), xq[h])
            nc.scalar.copy(y[t][:, HALF * h : HALF * h + HALF], acc[:, 0:HALF])

        w2g = [on_vector([P, 4, HALF // 4, 4], BF16, f"w2g{h}") for h in range(2)]

        def round_w2(engine_copy, i, walk):
            a, n = w2_cuts[i]
            h, first = divmod(a, HALF)
            engine_copy(
                w2g[h][:, :, first // 4 : (first + n) // 4, :].rearrange("p t m j -> " + walk),
                w2_raw[i][:].rearrange("p j (m t) -> " + walk, t=4),
            )

        w2q = (keep.tile([P, H], U32, name="w2_codes", align_bytes=64), keep.tile([P, H], U8, name="w2_scales", align_bytes=64))

        def quantise_w2(h, planes_wanted):
            for t in planes_wanted:
                quantise(*columns(w2q, P * t + 64 * h, 64), w2g[h][:, t, :, :].rearrange("p m j -> p (m j)"))

        round_w2(vector_copy, 0, "p m j t")
        round_w2(vector_copy, 1, "p m j t")
        quantise_w2(0, range(4))
        round_w2(gpsimd_copy, 2, "p t m j")

        o_scales = keep.tile([P, S], U8, name="o_scales", align_bytes=64)
        out0_v = out_0.rearrange("(p t) j -> p t j", t=4)
        out1_v = out_1[0].rearrange("p n t -> p (n t)").bitcast(I32)
        z, zb, zq, z_t, u_t, eq, o_t, back, outs, kept, moved, ob, o_codes, work = ({} for i in range(14))

        def planes(tile):
            return tile[:].rearrange("p (t j) -> p t j", t=4)

        def along_cells(row, q):
            first = LEAD + (q - TURNED) * P
            return row[:, first : first + P].unsqueeze(1).to_broadcast([P, 4, P])

        def interleave(engine_copy, dst, src):
            engine_copy(dst.rearrange("p (c i) t -> p c t i", i=4), src.rearrange("p t (c i) -> p c t i", i=4))

        def gather(engine_copy, dst, t, first, count):
            engine_copy(dst[:, t, :], y[t][:].indirect(stream_t[:, 8 * first : 8 * (first + count)]))

        def round_z(engine_copy, make, q):
            work[q] = make([P, 4 * P], F32, f"work{q}")
            zb[q] = work[q][:].bitcast(BF16)[:, 0 : 4 * P]
            interleave(engine_copy, zb[q].rearrange("p (n t) -> p n t", t=4), z[q])

        def quantise_z(q):
            zq[q] = (on_vector([P, P], U32, f"z_codes{q}")[:], keep.tile([P, P], U8, name=f"z_scales{q}", align_bytes=64)[:])
            quantise(*zq[q], zb[q])

        def turn_z(q):
            z_t[q] = bank()
            for t in range(4):
                nc.tensor.transpose(z_t[q][:, P * t : P * t + P], z[q][:, t, :], ident[:])

        def kept_turned(q):
            u_t[q] = on_scalar([P, 512], F32, f"u_t{q}")
            nc.scalar.activation(u_t[q][:], z_t[q][:], COPY, scale=stay[:, LEAD - TURNED + q : LEAD - TURNED + q + 1])

        def product_turned(q):
            eq[q] = bank()
            product(eq[q][:], zq[q], (w2q[0][:], w2q[1][:]))

        def product_planes(q):
            eq[q] = bank()
            for t in range(4):
                product(eq[q][:, P * t : P * t + P], columns(w2q, P * t, P), zq[q])

        def relax_turned(q):
            o_t[q] = [on_vector([P, HALF], F32, f"o_t{q}{e}") for e in range(2)]
            for e in range(2):
                cols = slice(HALF * e, HALF * e + HALF)
                nc.vector.scalar_tensor_tensor(
                    o_t[q][e][:], eq[q][:, cols], rate[:, LEAD - TURNED + q : LEAD - TURNED + q + 1], u_t[q][:, cols], MULT, ADD
                )

        def turn_back(q):
            back[q] = [bank() for e in range(2)]
            for t in range(4):
                nc.tensor.transpose(back[q][t // 2][:, P * (t % 2) : P * (t % 2) + P], o_t[q][t // 2][:, P * (t % 2) : P * (t % 2) + P], ident[:])

        def leave_psum(q):
            for e in range(2):
                nc.scalar.copy(outs[q][:, 2 * e : 2 * e + 2, :], back[q][e][:, 0:HALF].rearrange("p (t j) -> p t j", t=2))

        def kept_on_gpsimd(q):
            kept[q] = planes(work[q])
            nc.gpsimd.tensor_tensor(kept[q], z[q], along_cells(stay, q), MULT)

        def moved_planes(q):
            moved[q] = on_vector([P, 4, P], F32, f"moved{q}")
            nc.vector.tensor_tensor(moved[q][:], planes(eq[q]), along_cells(rate, q), MULT)

        def round_planes(engine_copy, make, q):
            ob[q] = make([P, P, 4], BF16, f"ob{q}")
            interleave(engine_copy, ob[q][:], outs[q])

        def quantise_out(q, first, last):
            if q == first:
                o_codes[first] = on_vector([P, P * (last + 1 - first)], I32, f"o_codes{first}")
            at = P * (q - first)
            quantise(o_codes[first][:, at : at + P], o_scales[:, P * q : P * q + P], ob[q][:].rearrange("p n t -> p (n t)"))
            if q == last:
                nc.sync.dma_start(out1_v[:, P * first : P * last + P], o_codes[first][:])

        z01 = on_vector([P, 4, HALF], F32, "z01")
        z[0], z[1] = z01[:, :, 0:P], z01[:, :, P:HALF]
        for t in range(3):
            gather(vector_copy, z01, t, 0, 2)
        gather(vector_copy, z[0], 3, 0, 1)
        z[2] = on_scalar([P, 4, P], F32, "z2")[:]
        gather(scalar_copy, z[2], 0, 2, 1)
        gather(scalar_copy, z[1], 3, 1, 1)
        gather(scalar_copy, z[2], 1, 2, 1)
        gather(scalar_copy, z[2], 2, 2, 1)
        stay = on_scalar([P, LEAD + P], F32, "stay")
        nc.scalar.activation(stay[:, LEAD - TURNED :], rate[:, LEAD - TURNED : LEAD + P], COPY, scale=-1.0, bias=1.0)
        gather(scalar_copy, z[2], 3, 2, 1)
        quantise_w2(1, range(3))
        round_z(vector_copy, on_vector, 0)
        round_z(vector_copy, on_vector, 1)
        turn_z(0)
        turn_z(1)
        quantise_z(0)
        quantise_w2(1, range(3, 4))
        quantise_z(1)
        kept_turned(0)
        kept_turned(1)
        product_turned(0)
        product_turned(1)
        round_z(vector_copy, on_vector, 2)
        z[3] = on_vector([P, 4, P], F32, "z3")[:]
        gather(vector_copy, z[3], 0, 3, 1)
        quantise_z(2)
        gather(scalar_copy, z[3], 2, 3, 1)
        gather(scalar_copy, z[3], 3, 3, 1)
        kept_on_gpsimd(2)
        product_planes(2)
        relax_turned(0)
        gather(vector_copy, z[3], 1, 3, 1)
        round_z(nc.scalar.copy, on_scalar, 3)
        relax_turned(1)
        turn_back(0)
        turn_back(1)
        moved_planes(2)
        quantise_z(3)
        pairs = [slice(2 * e, 2 * e + 2) for e in range(2)]
        eq3 = [bank() for e in range(2)]
        for t in range(4):
            product(eq3[t // 2][:, P * (t % 2) : P * (t % 2) + P], columns(w2q, P * t, P), zq[3])

        def lost_pair(e):
            kept[3, e] = on_vector([P, 2, P], F32, f"lost3{e}")
            nc.vector.scalar_tensor_tensor(kept[3, e][:], along_cells(rate, 3)[:, pairs[e], :], 1.0, z[3][:, pairs[e], :], SUBTRACT, MULT)

        lost_pair(0)
        outs[0] = on_scalar([P, 4, P], F32, "o0")[:]
        leave_psum(0)
        for e in range(2):
            nc.sync.dma_start(out0_v[:, 2 * e : 2 * e + 2, 0:P], outs[0][:, 2 * e : 2 * e + 2, :])
        o12 = on_vector([P, 4, HALF], F32, "o12")
        outs[1], outs[2] = o12[:, :, 0:P], o12[:, :, P:HALF]
        nc.vector.tensor_tensor(outs[2], moved[2][:], kept[2], ADD)
        leave_psum(1)
        nc.sync.dma_start(out0_v[:, :, P : P + HALF], o12[:])
        lost_pair(1)
        for q in range(3):
            round_planes(nc.scalar.copy, on_scalar, q)
        moved3 = [on_vector([P, 2, P], F32, f"moved3{e}") for e in range(2)]
        for e in range(2):
            pair = eq3[e][:, 0:HALF].rearrange("p (t j) -> p t j", t=2)
            nc.vector.tensor_tensor(moved3[e][:], pair, along_cells(rate, 3)[:, pairs[e], :], MULT)
        outs[3] = on_vector([P, 4, P], F32, "o3")[:]
        for e in range(2):
            nc.vector.tensor_tensor(outs[3][:, pairs[e], :], moved3[e][:], kept[3, e][:], SUBTRACT)
        nc.sync.dma_start(out0_v[:, :, 3 * P : S], outs[3])
        quantise_out(0, 0, 1)
        quantise_out(1, 0, 1)
        round_planes(vector_copy, on_vector, 3)
        quantise_out(2, 2, 3)
        quantise_out(3, 2, 3)
        for r in range(4):
            (nc.scalar, nc.sync)[r % 2].dma_start(out_2[0, r:16:4, :].bitcast(I32), o_scales[r:P:32, :].bitcast(I32))
